import numpy as np
import ml_dtypes


def mxq(x, axis, fmt="e4m3"):
    dtype, down = {"e4m3": (ml_dtypes.float8_e4m3fn, 7), "e5m2": (ml_dtypes.float8_e5m2, 14)}[fmt]
    v = np.moveaxis(np.asarray(x, np.float32).astype(ml_dtypes.bfloat16).astype(np.float64), axis, -1)
    blocks = v.reshape(v.shape[:-1] + (-1, 32))
    amax = np.abs(blocks).max(-1, keepdims=True)
    byte = np.maximum(np.where(amax > 0, np.frexp(amax)[1] - 1 + 127, 0) - down, 1)
    scale = np.exp2(byte - 127.0)
    codes = (blocks / scale).astype(np.float32).astype(dtype).astype(np.float64)
    return np.moveaxis((codes * scale).reshape(v.shape), -1, axis)


WIDE = False


def mx_kscale(k):
    if not WIDE:
        return np.ones(k)
    levels = np.array([10, -10, 5, -5, 0])
    if k % 512:
        return np.exp2(np.random.permutation(np.resize(levels, k // 32))).repeat(32)
    a = np.empty((k // 512, 16))
    for p in range(k // 512):
        a[p, :8] = np.random.permutation(np.resize(levels, 8))
        for g in range(8):
            far = levels[np.abs(levels - a[p, g]) >= 10]
            a[p, g + 8] = far[np.random.randint(len(far))]
    return np.exp2(a.ravel()).repeat(32)


BF16 = ml_dtypes.bfloat16


def bf(x):
    return np.asarray(x, np.float32).astype(BF16)


def f64(x):
    return np.asarray(x).astype(np.float64)


E2M1 = np.array([0.0, 0.5, 1.0, 1.5, 2.0, 3.0, 4.0, 6.0, -0.0, -0.5, -1.0, -1.5, -2.0, -3.0, -4.0, -6.0])


def pack_weight(w, fmt):
    k, n = w.shape
    w = f64(bf(w)).reshape(k // 32, 32, n)
    amax = np.abs(w).max(1)
    if fmt == "e4m3":
        byte = np.frexp(amax)[1] - 1 + 127 - 7
    else:
        mant, ex = np.frexp(amax / 6.0)
        byte = np.where(mant > 0.5, ex, ex - 1) + 127
    byte = np.clip(np.where(amax > 0, byte, 1), 1, 254)
    scaled = (w * np.exp2(127.0 - byte)[:, None, :]).reshape(k, n).astype(np.float32)
    by_word = np.ascontiguousarray(scaled.reshape(k // 512, 128, 4, n).transpose(0, 1, 3, 2))
    if fmt == "e4m3":
        words = by_word.astype(ml_dtypes.float8_e4m3fn).view(np.uint8)
    else:
        c = by_word.astype(ml_dtypes.float4_e2m1fn).view(np.uint8) & 0xF
        words = c[..., 0::2] | (c[..., 1::2] << 4)
    return np.ascontiguousarray(words), np.ascontiguousarray(byte.astype(np.uint8).reshape(k // 512, 16, n))


def unpack_weight(words, scales, fmt):
    g, p, n, _ = words.shape
    if fmt == "e4m3":
        vals = np.ascontiguousarray(words).view(ml_dtypes.float8_e4m3fn).astype(np.float64)
    else:
        nib = np.empty((g, p, n, 4), np.uint8)
        nib[..., 0::2] = words & 0xF
        nib[..., 1::2] = words >> 4
        vals = E2M1[nib]
    vals = vals * np.repeat(np.exp2(scales.astype(np.float64) - 127.0), 8, axis=1)[..., None]
    return vals.transpose(0, 1, 3, 2).reshape(g * 512, n)
def pack4(w):
    words, scales = pack_weight(w, "e2m1")
    return words.reshape(words.shape[0], 128, -1), scales


def unpack4(words, scales):
    return unpack_weight(words.reshape(words.shape[0], 128, -1, 2), scales, "e2m1")


def planes(Y):
    n, m = Y.shape
    b = f64(bf(Y)).reshape(n // 32, 32, m)
    amax = np.abs(b).max(1)
    byte = np.clip(np.where(amax > 0, np.frexp(amax)[1] - 1 + 127 - 7, 1), 1, 254)
    codes = (b * np.exp2(127.0 - byte)[:, None, :]).reshape(n, m).astype(np.float32).astype(ml_dtypes.float8_e4m3fn).view(np.uint8)
    words = codes.reshape(n // 512, 128, 4, m).transpose(0, 1, 3, 2)
    return np.ascontiguousarray(words), np.ascontiguousarray(byte.astype(np.uint8).reshape(n // 512, 16, m))


C, T, F, L, R = 2, 1024, 1024, 512, 1024

def setup_inputs():
    rn = np.random.standard_normal
    s_l, s_r, t_f = mx_kscale(L), mx_kscale(R), mx_kscale(F)
    x = rn((L, T)) * s_l[:, None]
    enc = rn((L, F)) / np.sqrt(L) / s_l[:, None] * t_f[None, :]
    mix = 3.0 * rn((F, R)) / np.sqrt(F * R) * s_r[None, :] / t_f[:, None]
    atoms = rn((R, L)) / s_r[:, None]
    x_words, x_scales = pack_weight(x, "e4m3")
    atoms_words, atoms_scales = pack4(atoms)
    return {"x_words": x_words, "x_scales": x_scales, "enc": bf(enc),
            "mask": bf(1.0 / (1.0 + np.exp(-1.5 * rn((C, T, F))))),
            "mix": bf(mix), "atoms_words": atoms_words, "atoms_scales": atoms_scales,
            "gain": bf(np.exp(0.8 * rn(L))), "bias": bf(0.4 * rn(L)),
            "level": bf(np.exp(0.3 * rn(T)))}

def reference(x_words, x_scales, enc, mask, mix, atoms_words, atoms_scales, gain, bias, level):
    x = unpack_weight(x_words, x_scales, "e4m3")
    a = unpack4(atoms_words, atoms_scales)
    w = np.maximum(x.T @ mxq(f64(enc), 0, "e4m3"), 0.0)
    h = (f64(mask) * w[None, :, :]).reshape(C * T, F)
    b = mxq(f64(mix), 1, "e4m3") @ a
    est = (mxq(h, 1, "e4m3") @ mxq(b, 0, "e4m3")).reshape(C, T, L)
    y = (est * f64(gain)[None, None, :] + f64(bias)[None, None, :]) * f64(level)[None, :, None]
    Y = y.reshape(C * T, L).T
    words, scales = planes(Y)
    return y, words, scales

@@ -1,0 +1,590 @@
+from contextlib import ExitStack
+
+import concourse.mybir as mybir
+from concourse.masks import make_identity
+
+C, T, F, L, R = 2, 1024, 1024, 512, 1024
+FLOPS = 2 * (T * F * L + F * L * R + C * T * L * F)
+
+F32 = mybir.dt.float32
+BF16 = mybir.dt.bfloat16
+I32 = mybir.dt.int32
+U32 = mybir.dt.uint32
+U8 = mybir.dt.uint8
+FP8X4 = mybir.dt.float8_e4m3fn_x4
+FP4X4 = mybir.dt.float4_e2m1fn_x4
+ALU = mybir.AluOpType
+ACT = mybir.ActivationFunctionType
+
+P = 128
+NT = T // P
+ENC_SPLIT = 88
+LATE = 5
+
+
+def tile_masked_frame_decode_k4_kernel(
+    tc, x_words, x_scales, enc, mask, mix, atoms_words, atoms_scales, gain, bias, level, out_0, out_1, out_2
+):
+    nc = tc.nc
+    with ExitStack() as ctx:
+        keep = ctx.enter_context(tc.tile_pool(name="keep", bufs=1))
+        ring = ctx.enter_context(tc.tile_pool(name="ring", bufs=3))
+        psum = ctx.enter_context(tc.psum_pool(name="psum", bufs=1))
+        ctx.enter_context(tc.manual_schedule())
+
+        def kept(name, shape, dtype):
+            return keep.tile(shape, dtype, name=name, align_bytes=64)
+
+        bank = [psum.tile([P, 512], F32, name="bank%d" % i) for i in range(8)]
+        w_bank, ht_bank, est_bank, yt_bank = bank[0:2], bank[2:4], bank[4:6], bank[6:8]
+        spare_bank = bank[4:8]
+
+        ident32 = kept("ident32", [P, P], F32)
+        ident16 = kept("ident16", [P, P], BF16)
+        in_scales = kept("in_scales", [P, 2048], U8)
+        x_scale = in_scales[:, 0:T]
+        atom_scale = in_scales[:, T : T + 2 * L].rearrange("p (g n) -> p g n", g=2)
+        x_codes = kept("x_codes", [P, T], U32)
+        atom_codes = kept("atom_codes", [P, 2, 2 * L], U8)
+        enc_raw = kept("enc_raw", [P, 4, F], BF16)
+        enc_b = kept("enc_b", [P, 2, 256, 2, 4], BF16)
+        enc_codes = kept("enc_codes", [P, F], U32)
+        enc_scale = kept("enc_scale", [P, F], U8)
+        mask_sb = kept("mask_sb", [P, NT, C, F], BF16)
+        mix_raw = kept("mix_raw", [P, 2, 4, R], BF16)
+        mix_b = kept("mix_b", [P, 2, 2, 2048], BF16)
+        mix_codes = kept("mix_codes", [P, 2, 2, 512], U32)
+        mix_scale = kept("mix_scale", [P, 2, 2, 512], U8)
+        basis_b = kept("basis_b", [P, 2, 2048], BF16)
+        basis_codes = kept("basis_codes", [P, 2, 512], U32)
+        basis_scale = kept("basis_scale", [P, 2, 512], U8)
+        h_codes = kept("h_codes", [P, NT, 512], U32)
+        h_scale = kept("h_scale", [P, NT, 512], U8)
+        y_codes = kept("y_codes", [P, C * T], U32)
+        y_scale = kept("y_scale", [P, C * T], U8)
+        gain_raw = kept("gain_raw", [P, 4], BF16)
+        bias_raw = kept("bias_raw", [P, 4], BF16)
+        gain32 = kept("gain32", [P, 4], F32)
+        bias32 = kept("bias32", [P, 4], F32)
+        level_rows = kept("level_rows", [P, P], BF16)
+        level_col16 = kept("level_col16", [P, NT], BF16)
+        level_col = kept("level_col", [P, NT], F32)
+        level_all = kept("level_all", [P, T], F32)
+        h_tiles, ht_tiles, z_tiles, yb_tiles, y_tiles = {}, {}, {}, {}, {}
+
+        x_dram = x_words[0].rearrange("p n t -> p (n t)").bitcast(I32)
+        codes_dram = out_1[0].rearrange("p m t -> p (m t)").bitcast(I32).rearrange("p (c i) -> p c i", c=C)
+
+        def load_enc(g):
+            cols = slice(512 * g, 512 * (g + 1))
+            nc.sync.dma_start(out=enc_raw[:, :, cols], in_=enc[:, cols].rearrange("(p j) f -> p j f", j=4))
+
+        def load_x(lo, hi):
+            nc.sync.dma_start(out=x_codes[:, lo:hi].bitcast(I32), in_=x_dram[:, lo:hi])
+
+        def load_mask(j):
+            nc.sync.dma_start(out=mask_sb[:, j], in_=mask[:, P * j : P * (j + 1), :].rearrange("c i f -> i c f"))
+
+        def load_mix(g, half):
+            rows = mix[512 * g : 512 * (g + 1), :].rearrange("(m t) k -> m t k", t=4)
+            nc.sync.dma_start(out=mix_raw[:, g, 2 * half : 2 * half + 2, :], in_=rows[:, 2 * half : 2 * half + 2, :])
+
+        def load_atoms():
+            nc.sync.dma_start(out=atom_codes[:].bitcast(I32), in_=atoms_words.rearrange("g p n -> p g n").bitcast(I32))
+
+        def load_x_scales(q):
+            nc.sync.dma_start(
+                out=x_scale[32 * q : 32 * q + 4, :].bitcast(I32), in_=x_scales[0, 4 * q : 4 * q + 4, :].bitcast(I32)
+            )
+
+        def load_atom_scales(q):
+            nc.sync.dma_start(
+                out=atom_scale[32 * q : 32 * q + 4].bitcast(I32),
+                in_=atoms_scales[:, 4 * q : 4 * q + 4, :].rearrange("g r n -> r g n").bitcast(I32),
+            )
+
+        def copy_on(on_vector, dst, src):
+            if on_vector:
+                nc.vector.tensor_copy(out=dst, in_=src)
+            else:
+                nc.scalar.copy(out=dst, in_=src)
+
+        def spread_level():
+            col_ps = yt_bank[0][:].bitcast(BF16)
+            nc.tensor.transpose(col_ps[:, 0:P], level_rows[:], ident16[:])
+            nc.scalar.activation(out=level_col[:], in_=col_ps[:, 0:NT], func=ACT.Identity)
+            nc.scalar.copy(out=level_col16[:], in_=col_ps[:, 0:NT])
+            all_ps = yt_bank[1][:].bitcast(BF16)
+            for j in range(NT):
+                nc.tensor.transpose(
+                    all_ps[:, P * j : P * (j + 1)], level_col16[:, j : j + 1].to_broadcast([P, P]), ident16[:]
+                )
+            nc.scalar.copy(out=level_all[:], in_=all_ps)
+
+        def enc_interleave(on_vector, g, u):
+            lo, hi = (128 * g, 128 * g + ENC_SPLIT) if on_vector else (128 * g + ENC_SPLIT, 128 * (g + 1))
+            src = enc_raw[:].rearrange("p j (m u e) -> p u m j e", u=2, e=2)[:, u, lo:hi]
+            dst = enc_b[:, u, lo:hi].rearrange("p m e j -> p m j e")
+            if on_vector:
+                nc.vector.tensor_copy(out=dst, in_=src)
+            else:
+                nc.scalar.copy(out=dst, in_=src)
+
+        def quantize(codes, scales, values):
+            nc.vector.quantize_mx(out=codes.bitcast(FP8X4), scales=scales, in_=values)
+
+        def enc_quantize(g, u):
+            cols = slice(512 * u + 256 * g, 512 * u + 256 * (g + 1))
+            values = enc_b[:, u, 128 * g : 128 * (g + 1)].rearrange("p m e j -> p (m e j)")
+            quantize(enc_codes[:, cols], enc_scale[:, cols], values)
+
+        def mix_transpose(g, t):
+            words = mix_raw[:, g, t, :].bitcast(F32)
+            for kg in range(2):
+                for u in range(2):
+                    n = 2 * kg + u
+                    nc.tensor.transpose(
+                        spare_bank[t][:, P * n : P * (n + 1)], words[:, 256 * kg + u : 256 * (kg + 1) : 2], ident32[:]
+                    )
+
+        def mix_copy(g, t, on_vector=False):
+            dst = mix_b[:, g].bitcast(F32).rearrange("p k (t f u) -> p t k f u", t=4, u=2)[:, t]
+            copy_on(on_vector, dst, spare_bank[t][:].rearrange("p (k u f) -> p k f u", k=2, u=2))
+
+        def mix_quantize(g, kg):
+            quantize(mix_codes[:, g, kg], mix_scale[:, g, kg], mix_b[:, g, kg])
+
+        def basis_matmul(g, lq):
+            for t in range(4):
+                for kg in range(2):
+                    nc.tensor.matmul_mx(
+                        out=spare_bank[lq][:, P * t : P * (t + 1)],
+                        lhsT=mix_codes[:, g, kg, P * t : P * (t + 1)].bitcast(FP8X4),
+                        lhsT_scale=mix_scale[:, g, kg, P * t : P * (t + 1)],
+                        rhs=atom_codes[:, kg, 256 * lq : 256 * (lq + 1)].bitcast(FP4X4),
+                        rhs_scale=atom_scale[:, kg, P * lq : P * (lq + 1)],
+                        start=(kg == 0),
+                        stop=(kg == 1),
+                    )
+
+        def basis_copy(g, lq, on_vector=False):
+            dst = basis_b[:, g].rearrange("p (s m t) -> p s m t", s=4, t=4)[:, :, 32 * lq : 32 * (lq + 1), :]
+            copy_on(on_vector, dst, spare_bank[lq][:].rearrange("p (t m s) -> p s m t", t=4, s=4))
+
+        def basis_quantize(g):
+            quantize(basis_codes[:, g], basis_scale[:, g], basis_b[:, g])
+
+        def w_matmul(j, u):
+            frames = slice(P * j, P * (j + 1))
+            for u in (u,):
+                cols = slice(512 * u, 512 * (u + 1))
+                nc.tensor.matmul_mx(
+                    out=w_bank[u][:],
+                    lhsT=x_codes[:, frames].bitcast(FP8X4),
+                    lhsT_scale=x_scale[:, frames],
+                    rhs=enc_codes[:, cols].bitcast(FP8X4),
+                    rhs_scale=enc_scale[:, cols],
+                    start=True,
+                    stop=True,
+                )
+
+        def h_multiply(j, c, u):
+            if c == 0 and u == 0:
+                h_tiles[j] = ring.tile([P, C, 2, 512], BF16, name="h_rows", bufs=3, align_bytes=64)
+            for u in (u,):
+                nc.vector.scalar_tensor_tensor(
+                    out=h_tiles[j][:, c, u].rearrange("p (m e) -> p m e", e=2),
+                    in0=w_bank[u][:].rearrange("p (m e) -> p m e", e=2),
+                    scalar=0.0,
+                    in1=mask_sb[:, j, c].rearrange("p (m u e) -> p u m e", u=2, e=2)[:, u],
+                    op0=ALU.max,
+                    op1=ALU.mult,
+                )
+
+        def h_transpose(j, c):
+            for g in range(2):
+                for u in range(2):
+                    n = 2 * g + u
+                    words = h_tiles[j][:, c, u].bitcast(F32)
+                    nc.tensor.transpose(ht_bank[c][:, P * n : P * (n + 1)], words[:, P * g : P * (g + 1)], ident32[:])
+
+        def h_copy(j, c, on_vector=False):
+            if c == 0:
+                ht_tiles[j] = ring.tile([P, 2048], BF16, name="h_cols", align_bytes=64)
+            dst = ht_tiles[j][:].bitcast(F32).rearrange("p (g c i u) -> p c g i u", g=2, c=C, u=2)[:, c]
+            copy_on(on_vector, dst, ht_bank[c][:].rearrange("p (g u i) -> p g i u", g=2, u=2))
+
+        def h_quantize(j):
+            quantize(h_codes[:, j], h_scale[:, j], ht_tiles[j][:])
+
+        def est_banks(j):
+            return w_bank if j >= LATE and (j - LATE) % 2 == 0 else est_bank
+
+        def yt_banks(j):
+            return ht_bank if j >= LATE and (j - LATE) % 2 == 0 else yt_bank
+
+        def est_matmul(j, half):
+            for s in range(2 * half, 2 * half + 2):
+                for g in range(2):
+                    nc.tensor.matmul_mx(
+                        out=est_banks(j)[s // 2][:, 256 * (s % 2) : 256 * (s % 2 + 1)],
+                        lhsT=basis_codes[:, g, P * s : P * (s + 1)].bitcast(FP8X4),
+                        lhsT_scale=basis_scale[:, g, P * s : P * (s + 1)],
+                        rhs=h_codes[:, j, 256 * g : 256 * (g + 1)].bitcast(FP8X4),
+                        rhs_scale=h_scale[:, j, 256 * g : 256 * (g + 1)],
+                        start=(g == 0),
+                        stop=(g == 1),
+                    )
+
+        def z_affine(j, half, on_vector=False):
+            if half == 0:
+                z_tiles[j] = ring.tile([P, 4, 256], F32, name="z", bufs=5, align_bytes=64)
+            for s in range(2 * half, 2 * half + 2):
+                src = est_banks(j)[s // 2][:, 256 * (s % 2) : 256 * (s % 2 + 1)]
+                scale, shift = gain32[:, s : s + 1], bias32[:, s : s + 1]
+                if on_vector:
+                    nc.vector.tensor_scalar(
+                        out=z_tiles[j][:, s], in0=src, scalar1=scale, scalar2=shift, op0=ALU.mult, op1=ALU.add
+                    )
+                else:
+                    nc.scalar.activation(out=z_tiles[j][:, s], in_=src, func=ACT.Identity, scale=scale, bias=shift)
+
+        def y_round(j, c, on_vector):
+            if c == 0:
+                yb_tiles[j] = ring.tile([P, C, 512], BF16, name="y_b", bufs=4, align_bytes=64)
+            lev = level_all[:, P * j : P * (j + 1)]
+            dst, src = yb_tiles[j][:, c], z_tiles[j][:, :, P * c : P * (c + 1)]
+            if on_vector:
+                nc.vector.tensor_tensor(
+                    out=dst.rearrange("p (a i s) -> p a s i", i=2, s=4),
+                    in0=src.rearrange("p s (a i) -> p a s i", i=2),
+                    in1=lev.rearrange("p (a i) -> p a i", i=2).unsqueeze(2).broadcast_to([P, P // 2, 4, 2]),
+                    op=ALU.mult,
+                )
+            else:
+                nc.gpsimd.tensor_tensor(
+                    out=dst.rearrange("p (i s) -> p i s", s=4),
+                    in0=src.rearrange("p s i -> p i s"),
+                    in1=lev.unsqueeze(2).broadcast_to([P, P, 4]),
+                    op=ALU.mult,
+                )
+
+        def y_quantize(j, c):
+            for c in (c,):
+                cols = slice(T * c + P * j, T * c + P * (j + 1))
+                quantize(y_codes[:, cols], y_scale[:, cols], yb_tiles[j][:, c])
+
+        def y_transpose(j, c):
+            for s in range(4):
+                nc.tensor.transpose(yt_banks(j)[c][:, P * s : P * (s + 1)], z_tiles[j][:, s, P * c : P * (c + 1)], ident32[:])
+
+        def y_copy(j, c, on_vector=False):
+            if c == 0:
+                y_tiles[j] = ring.tile([P, C, L], F32, name="y_rows", align_bytes=64)
+            dst = y_tiles[j][:, c].rearrange("p (m s) -> p m s", s=4)
+            src = yt_banks(j)[c][:].rearrange("p (s m) -> p m s", s=4)
+            if on_vector:
+                nc.vector.tensor_scalar(out=dst, in0=src, scalar1=level_col[:, j : j + 1], scalar2=None, op0=ALU.mult)
+            else:
+                nc.scalar.activation(out=dst, in_=src, func=ACT.Copy, scale=level_col[:, j : j + 1])
+
+        def store_y(j, lo, hi):
+            rows = out_0[lo:hi, P * j : P * (j + 1), :].rearrange("c i l -> i c l")
+            nc.sync.dma_start(out=rows, in_=y_tiles[j][:, lo:hi])
+
+        def store_codes(lo, hi):
+            src = y_codes[:].bitcast(I32).rearrange("p (c i) -> p c i", c=C)
+            nc.sync.dma_start(out=codes_dram[:, :, P * lo : P * hi], in_=src[:, :, P * lo : P * hi])
+
+        def store_scales(q, eng):
+            eng.dma_start(
+                out=out_2[0, 4 * q : 4 * q + 4, :].bitcast(I32), in_=y_scale[32 * q : 32 * q + 4, :].bitcast(I32)
+            )
+
+        load_enc(0)
+        nc.vector.memset(in_scales[:].bitcast(U32), 0)
+        nc.vector.memset(level_rows[:], 0.0)
+        load_atom_scales(0)
+        make_identity(nc, ident16[:])
+        load_x_scales(0)
+        load_atom_scales(1)
+        load_enc(1)
+        load_x_scales(1)
+        load_mix(0, 0)
+        load_x(0, 256)
+        nc.gpsimd.dma_start(out=level_rows[0:NT, :], in_=level.rearrange("(j p) -> j p", p=P))
+        make_identity(nc, ident32[:])
+        nc.gpsimd.dma_start(out=gain_raw[:], in_=gain.rearrange("(p s) -> p s", s=4))
+        enc_interleave(False, 0, 1)
+        enc_interleave(True, 0, 0)
+        load_x_scales(2)
+        load_mask(0)
+        load_x_scales(3)
+        load_mix(0, 1)
+        enc_interleave(False, 0, 0)
+        enc_interleave(True, 0, 1)
+        enc_quantize(0, 0)
+        enc_interleave(False, 1, 0)
+        enc_interleave(True, 1, 1)
+        load_mask(1)
+        load_x(256, 1024)
+        enc_interleave(False, 1, 1)
+        enc_interleave(True, 1, 0)
+        spread_level()
+        enc_quantize(0, 1)
+        load_mask(2)
+        enc_quantize(1, 0)
+        load_atoms()
+        enc_quantize(1, 1)
+        load_atom_scales(2)
+        nc.gpsimd.dma_start(out=bias_raw[:], in_=bias.rearrange("(p s) -> p s", s=4))
+        w_matmul(0, 0)
+        load_atom_scales(3)
+        load_mask(3)
+        w_matmul(0, 1)
+        h_multiply(0, 0, 0)
+        mix_transpose(0, 0)
+        h_multiply(0, 0, 1)
+        load_mix(1, 0)
+        mix_transpose(0, 1)
+        mix_copy(0, 0, False)
+        h_multiply(0, 1, 0)
+        mix_transpose(0, 2)
+        mix_copy(0, 1, False)
+        h_multiply(0, 1, 1)
+        load_mix(1, 1)
+        w_matmul(1, 0)
+        nc.scalar.activation(out=gain32[:], in_=gain_raw[:], func=ACT.Identity)
+        mix_copy(0, 2, False)
+        w_matmul(1, 1)
+        h_multiply(1, 0, 0)
+        h_transpose(0, 0)
+        load_mask(4)
+        h_multiply(1, 0, 1)
+        mix_transpose(0, 3)
+        h_copy(0, 0, False)
+        h_multiply(1, 1, 0)
+        h_transpose(0, 1)
+        mix_copy(0, 3, False)
+        load_mask(5)
+        h_multiply(1, 1, 1)
+        w_matmul(2, 0)
+        h_copy(0, 1, False)
+        load_mask(6)
+        h_transpose(1, 0)
+        mix_quantize(0, 0)
+        load_mask(7)
+        h_transpose(1, 1)
+        h_copy(1, 0, False)
+        mix_quantize(0, 1)
+        w_matmul(2, 1)
+        basis_matmul(0, 0)
+        h_multiply(2, 0, 0)
+        h_multiply(2, 0, 1)
+        basis_matmul(0, 1)
+        basis_copy(0, 0, False)
+        h_multiply(2, 1, 0)
+        basis_matmul(0, 2)
+        h_copy(1, 1, False)
+        h_multiply(2, 1, 1)
+        basis_copy(0, 1, False)
+        w_matmul(3, 0)
+        basis_matmul(0, 3)
+        h_quantize(0)
+        basis_copy(0, 2, False)
+        w_matmul(3, 1)
+        h_multiply(3, 0, 0)
+        basis_copy(0, 3, False)
+        mix_transpose(1, 0)
+        h_multiply(3, 0, 1)
+        mix_transpose(1, 1)
+        mix_copy(1, 0, False)
+        basis_quantize(0)
+        mix_transpose(1, 2)
+        mix_copy(1, 1, False)
+        h_multiply(3, 1, 0)
+        mix_transpose(1, 3)
+        mix_copy(1, 2, False)
+        h_quantize(1)
+        h_transpose(2, 0)
+        mix_copy(1, 3, False)
+        h_transpose(2, 1)
+        h_multiply(3, 1, 1)
+        w_matmul(4, 0)
+        h_copy(2, 0, False)
+        mix_quantize(1, 0)
+        w_matmul(4, 1)
+        h_copy(2, 1, False)
+        h_transpose(3, 0)
+        mix_quantize(1, 1)
+        nc.scalar.activation(out=bias32[:], in_=bias_raw[:], func=ACT.Identity)
+        basis_matmul(1, 0)
+        h_copy(3, 0, False)
+        h_multiply(4, 0, 0)
+        h_quantize(2)
+        basis_matmul(1, 1)
+        basis_copy(1, 0, False)
+        h_multiply(4, 0, 1)
+        basis_matmul(1, 2)
+        basis_copy(1, 1, False)
+        h_multiply(4, 1, 0)
+        basis_matmul(1, 3)
+        basis_copy(1, 2, False)
+        h_multiply(4, 1, 1)
+        w_matmul(5, 0)
+        basis_copy(1, 3, False)
+        h_transpose(3, 1)
+        h_multiply(5, 0, 0)
+        h_transpose(4, 0)
+        h_copy(3, 1, False)
+        basis_quantize(1)
+        w_matmul(5, 1)
+        h_copy(4, 0, False)
+        est_matmul(0, 0)
+        h_quantize(3)
+        est_matmul(0, 1)
+        h_multiply(5, 0, 1)
+        z_affine(0, 0, False)
+        h_transpose(4, 1)
+        h_multiply(5, 1, 0)
+        z_affine(0, 1, False)
+        est_matmul(1, 0)
+        h_multiply(5, 1, 1)
+        h_copy(4, 1, False)
+        est_matmul(1, 1)
+        y_round(0, 0, True)
+        z_affine(1, 0, False)
+        y_transpose(0, 0)
+        h_quantize(4)
+        z_affine(1, 1, False)
+        y_transpose(0, 1)
+        y_round(0, 1, True)
+        h_transpose(5, 0)
+        y_copy(0, 0, False)
+        w_matmul(6, 0)
+        y_quantize(0, 0)
+        y_round(1, 0, True)
+        h_copy(5, 0, False)
+        est_matmul(2, 0)
+        y_quantize(0, 1)
+        y_round(1, 1, True)
+        w_matmul(6, 1)
+        z_affine(2, 0, False)
+        est_matmul(2, 1)
+        h_multiply(6, 0, 0)
+        y_copy(0, 1, False)
+        h_transpose(5, 1)
+        h_multiply(6, 0, 1)
+        y_transpose(1, 0)
+        z_affine(2, 1, False)
+        store_y(0, 0, 2)
+        y_transpose(1, 1)
+        h_multiply(6, 1, 0)
+        est_matmul(3, 0)
+        y_copy(1, 0, False)
+        y_round(2, 0, True)
+        y_copy(1, 1, False)
+        est_matmul(3, 1)
+        y_round(2, 1, True)
+        z_affine(3, 0, False)
+        w_matmul(7, 0)
+        h_multiply(6, 1, 1)
+        h_transpose(6, 0)
+        h_copy(5, 1, False)
+        y_transpose(2, 0)
+        y_quantize(1, 0)
+        y_quantize(1, 1)
+        y_transpose(2, 1)
+        y_quantize(2, 0)
+        h_copy(6, 0, False)
+        store_codes(0, 2)
+        h_multiply(7, 0, 0)
+        store_y(1, 0, 2)
+        w_matmul(7, 1)
+        z_affine(3, 1, False)
+        y_quantize(2, 1)
+        est_matmul(4, 0)
+        h_multiply(7, 0, 1)
+        y_copy(2, 0, False)
+        h_transpose(6, 1)
+        h_quantize(5)
+        h_transpose(7, 0)
+        y_copy(2, 1, False)
+        y_round(3, 0, True)
+        y_transpose(3, 0)
+        h_copy(6, 1, False)
+        est_matmul(4, 1)
+        store_y(2, 0, 2)
+        h_multiply(7, 1, 0)
+        z_affine(4, 0, False)
+        y_transpose(3, 1)
+        h_multiply(7, 1, 1)
+        est_matmul(5, 0)
+        z_affine(4, 1, False)
+        y_quantize(3, 0)
+        h_quantize(6)
+        y_copy(3, 0, False)
+        est_matmul(5, 1)
+        z_affine(5, 0, True)
+        y_copy(3, 1, False)
+        h_transpose(7, 1)
+        h_copy(7, 0, True)
+        y_transpose(4, 0)
+        z_affine(5, 1, False)
+        store_y(3, 0, 2)
+        y_transpose(4, 1)
+        y_round(3, 1, True)
+        est_matmul(6, 0)
+        y_copy(4, 0, False)
+        y_round(4, 0, True)
+        y_copy(4, 1, False)
+        est_matmul(6, 1)
+        y_round(4, 1, True)
+        y_transpose(5, 0)
+        h_copy(7, 1, False)
+        y_quantize(3, 1)
+        y_quantize(4, 0)
+        store_codes(2, 4)
+        y_round(5, 0, True)
+        store_y(4, 0, 2)
+        z_affine(6, 0, False)
+        y_transpose(5, 1)
+        y_round(5, 1, True)
+        z_affine(6, 1, False)
+        y_transpose(6, 0)
+        y_quantize(4, 1)
+        y_quantize(5, 0)
+        y_copy(5, 0, False)
+        y_quantize(5, 1)
+        y_transpose(6, 1)
+        h_quantize(7)
+        store_codes(4, 6)
+        y_copy(5, 1, False)
+        y_round(6, 0, True)
+        est_matmul(7, 0)
+        y_copy(6, 0, False)
+        store_y(5, 0, 2)
+        y_round(6, 1, True)
+        est_matmul(7, 1)
+        y_copy(6, 1, False)
+        y_quantize(6, 0)
+        y_quantize(6, 1)
+        z_affine(7, 0, False)
+        z_affine(7, 1, True)
+        store_codes(6, 7)
+        store_y(6, 0, 2)
+        y_transpose(7, 0)
+        y_round(7, 0, True)
+        y_transpose(7, 1)
+        y_copy(7, 0, False)
+        y_round(7, 1, True)
+        y_copy(7, 1, False)
+        store_y(7, 0, 1)
+        y_quantize(7, 0)
+        y_quantize(7, 1)
+        store_y(7, 1, 2)
+        store_codes(7, 8)
+        store_scales(3, nc.scalar)
+        store_scales(1, nc.scalar)
+        store_scales(2, nc.sync)
+        store_scales(0, nc.sync)

@@ -18,8 +18,8 @@ ACT = mybir.ActivationFunctionType
 
 P = 128
 NT = T // P
-ENC_SPLIT = 88
-LATE = 5
+ENC_SPLIT = 80
+NUM_BANKS = 8
 
 
 def tile_masked_frame_decode_k4_kernel(
@@ -35,9 +35,17 @@ def tile_masked_frame_decode_k4_kernel(
         def kept(name, shape, dtype):
             return keep.tile(shape, dtype, name=name, align_bytes=64)
 
-        bank = [psum.tile([P, 512], F32, name="bank%d" % i) for i in range(8)]
-        w_bank, ht_bank, est_bank, yt_bank = bank[0:2], bank[2:4], bank[4:6], bank[6:8]
-        spare_bank = bank[4:8]
+        free_banks = [psum.tile([P, 512], F32, name="bank%d" % i) for i in range(NUM_BANKS)]
+        held = {}
+
+        def take_bank(key):
+            held[key] = free_banks[0]
+            free_banks.remove(held[key])
+            return held[key]
+
+        def give_bank(key):
+            free_banks.append(held[key])
+            return held[key]
 
         ident32 = kept("ident32", [P, P], F32)
         ident16 = kept("ident16", [P, P], BF16)
@@ -109,26 +117,29 @@ def tile_masked_frame_decode_k4_kernel(
             else:
                 nc.scalar.copy(out=dst, in_=src)
 
-        def spread_level():
-            col_ps = yt_bank[0][:].bitcast(BF16)
-            nc.tensor.transpose(col_ps[:, 0:P], level_rows[:], ident16[:])
-            nc.scalar.activation(out=level_col[:], in_=col_ps[:, 0:NT], func=ACT.Identity)
-            nc.scalar.copy(out=level_col16[:], in_=col_ps[:, 0:NT])
-            all_ps = yt_bank[1][:].bitcast(BF16)
+        def level_transpose():
+            nc.tensor.transpose(take_bank("level_col")[:].bitcast(BF16)[:, 0:P], level_rows[:], ident16[:])
+
+        def level_columns():
+            col_ps = give_bank("level_col")[:].bitcast(BF16)[:, 0:NT]
+            nc.scalar.copy(out=level_col16[:], in_=col_ps)
+            nc.scalar.activation(out=level_col[:], in_=col_ps, func=ACT.Identity)
+
+        def level_spread():
+            all_ps = take_bank("level_all")[:].bitcast(BF16)
             for j in range(NT):
                 nc.tensor.transpose(
                     all_ps[:, P * j : P * (j + 1)], level_col16[:, j : j + 1].to_broadcast([P, P]), ident16[:]
                 )
-            nc.scalar.copy(out=level_all[:], in_=all_ps)
 
-        def enc_interleave(on_vector, g, u):
+        def level_copy():
+            nc.scalar.copy(out=level_all[:], in_=give_bank("level_all")[:].bitcast(BF16))
+
+        def enc_interleave(on_vector, g):
             lo, hi = (128 * g, 128 * g + ENC_SPLIT) if on_vector else (128 * g + ENC_SPLIT, 128 * (g + 1))
-            src = enc_raw[:].rearrange("p j (m u e) -> p u m j e", u=2, e=2)[:, u, lo:hi]
-            dst = enc_b[:, u, lo:hi].rearrange("p m e j -> p m j e")
-            if on_vector:
-                nc.vector.tensor_copy(out=dst, in_=src)
-            else:
-                nc.scalar.copy(out=dst, in_=src)
+            src = enc_raw[:].rearrange("p j (m u e) -> p m j u e", u=2, e=2)[:, lo:hi]
+            dst = enc_b[:, :, lo:hi].rearrange("p u m e j -> p m j u e")
+            copy_on(on_vector, dst, src)
 
         def quantize(codes, scales, values):
             nc.vector.quantize_mx(out=codes.bitcast(FP8X4), scales=scales, in_=values)
@@ -140,25 +151,25 @@ def tile_masked_frame_decode_k4_kernel(
 
         def mix_transpose(g, t):
             words = mix_raw[:, g, t, :].bitcast(F32)
+            ps = take_bank(("mix", g, t))
             for kg in range(2):
                 for u in range(2):
                     n = 2 * kg + u
-                    nc.tensor.transpose(
-                        spare_bank[t][:, P * n : P * (n + 1)], words[:, 256 * kg + u : 256 * (kg + 1) : 2], ident32[:]
-                    )
+                    nc.tensor.transpose(ps[:, P * n : P * (n + 1)], words[:, 256 * kg + u : 256 * (kg + 1) : 2], ident32[:])
 
         def mix_copy(g, t, on_vector=False):
             dst = mix_b[:, g].bitcast(F32).rearrange("p k (t f u) -> p t k f u", t=4, u=2)[:, t]
-            copy_on(on_vector, dst, spare_bank[t][:].rearrange("p (k u f) -> p k f u", k=2, u=2))
+            copy_on(on_vector, dst, give_bank(("mix", g, t))[:].rearrange("p (k u f) -> p k f u", k=2, u=2))
 
         def mix_quantize(g, kg):
             quantize(mix_codes[:, g, kg], mix_scale[:, g, kg], mix_b[:, g, kg])
 
         def basis_matmul(g, lq):
+            ps = take_bank(("basis", g, lq))
             for t in range(4):
                 for kg in range(2):
                     nc.tensor.matmul_mx(
-                        out=spare_bank[lq][:, P * t : P * (t + 1)],
+                        out=ps[:, P * t : P * (t + 1)],
                         lhsT=mix_codes[:, g, kg, P * t : P * (t + 1)].bitcast(FP8X4),
                         lhsT_scale=mix_scale[:, g, kg, P * t : P * (t + 1)],
                         rhs=atom_codes[:, kg, 256 * lq : 256 * (lq + 1)].bitcast(FP4X4),
@@ -169,422 +180,383 @@ def tile_masked_frame_decode_k4_kernel(
 
         def basis_copy(g, lq, on_vector=False):
             dst = basis_b[:, g].rearrange("p (s m t) -> p s m t", s=4, t=4)[:, :, 32 * lq : 32 * (lq + 1), :]
-            copy_on(on_vector, dst, spare_bank[lq][:].rearrange("p (t m s) -> p s m t", t=4, s=4))
+            copy_on(on_vector, dst, give_bank(("basis", g, lq))[:].rearrange("p (t m s) -> p s m t", t=4, s=4))
 
         def basis_quantize(g):
             quantize(basis_codes[:, g], basis_scale[:, g], basis_b[:, g])
 
         def w_matmul(j, u):
             frames = slice(P * j, P * (j + 1))
-            for u in (u,):
-                cols = slice(512 * u, 512 * (u + 1))
-                nc.tensor.matmul_mx(
-                    out=w_bank[u][:],
-                    lhsT=x_codes[:, frames].bitcast(FP8X4),
-                    lhsT_scale=x_scale[:, frames],
-                    rhs=enc_codes[:, cols].bitcast(FP8X4),
-                    rhs_scale=enc_scale[:, cols],
-                    start=True,
-                    stop=True,
-                )
+            cols = slice(512 * u, 512 * (u + 1))
+            nc.tensor.matmul_mx(
+                out=take_bank(("w", j, u))[:],
+                lhsT=x_codes[:, frames].bitcast(FP8X4),
+                lhsT_scale=x_scale[:, frames],
+                rhs=enc_codes[:, cols].bitcast(FP8X4),
+                rhs_scale=enc_scale[:, cols],
+                start=True,
+                stop=True,
+            )
 
-        def h_multiply(j, c, u):
-            if c == 0 and u == 0:
-                h_tiles[j] = ring.tile([P, C, 2, 512], BF16, name="h_rows", bufs=3, align_bytes=64)
-            for u in (u,):
-                nc.vector.scalar_tensor_tensor(
-                    out=h_tiles[j][:, c, u].rearrange("p (m e) -> p m e", e=2),
-                    in0=w_bank[u][:].rearrange("p (m e) -> p m e", e=2),
-                    scalar=0.0,
-                    in1=mask_sb[:, j, c].rearrange("p (m u e) -> p u m e", u=2, e=2)[:, u],
-                    op0=ALU.max,
-                    op1=ALU.mult,
-                )
+        def h_multiply(j, u):
+            if u == 0:
+                h_tiles[j] = ring.tile([P, 2, C, 512], BF16, name="h_rows", align_bytes=64)
+            nc.vector.scalar_tensor_tensor(
+                out=h_tiles[j][:, u].rearrange("p c (m e) -> p c m e", e=2),
+                in0=give_bank(("w", j, u))[:].rearrange("p (m e) -> p m e", e=2).unsqueeze(1).broadcast_to([P, C, 256, 2]),
+                scalar=0.0,
+                in1=mask_sb[:, j].rearrange("p c (m u e) -> p u c m e", u=2, e=2)[:, u],
+                op0=ALU.max,
+                op1=ALU.mult,
+            )
 
         def h_transpose(j, c):
+            ps = take_bank(("h", j, c))
             for g in range(2):
                 for u in range(2):
                     n = 2 * g + u
-                    words = h_tiles[j][:, c, u].bitcast(F32)
-                    nc.tensor.transpose(ht_bank[c][:, P * n : P * (n + 1)], words[:, P * g : P * (g + 1)], ident32[:])
+                    words = h_tiles[j][:, u, c].bitcast(F32)
+                    nc.tensor.transpose(ps[:, P * n : P * (n + 1)], words[:, P * g : P * (g + 1)], ident32[:])
 
         def h_copy(j, c, on_vector=False):
-            if c == 0:
-                ht_tiles[j] = ring.tile([P, 2048], BF16, name="h_cols", align_bytes=64)
-            dst = ht_tiles[j][:].bitcast(F32).rearrange("p (g c i u) -> p c g i u", g=2, c=C, u=2)[:, c]
-            copy_on(on_vector, dst, ht_bank[c][:].rearrange("p (g u i) -> p g i u", g=2, u=2))
+            pair, half = j // 2, j % 2
+            if half == 0 and c == 0:
+                ht_tiles[pair] = ring.tile([P, 2, 2048], BF16, name="h_cols", bufs=2, align_bytes=64)
+            dst = ht_tiles[pair][:].bitcast(F32).rearrange("p g (c h i u) -> p c h g i u", c=C, h=2, u=2)[:, c, half]
+            copy_on(on_vector, dst, give_bank(("h", j, c))[:].rearrange("p (g u i) -> p g i u", g=2, u=2))
 
-        def h_quantize(j):
-            quantize(h_codes[:, j], h_scale[:, j], ht_tiles[j][:])
+        def h_quantize(pair, g):
+            quantize(h_codes[:, 2 * pair + g], h_scale[:, 2 * pair + g], ht_tiles[pair][:, g])
 
-        def est_banks(j):
-            return w_bank if j >= LATE and (j - LATE) % 2 == 0 else est_bank
+        def est_matmul(pair, s):
+            ps = take_bank(("est", pair, s))
+            for g in range(2):
+                nc.tensor.matmul_mx(
+                    out=ps[:],
+                    lhsT=basis_codes[:, g, P * s : P * (s + 1)].bitcast(FP8X4),
+                    lhsT_scale=basis_scale[:, g, P * s : P * (s + 1)],
+                    rhs=h_codes[:, 2 * pair + g].bitcast(FP8X4),
+                    rhs_scale=h_scale[:, 2 * pair + g],
+                    start=(g == 0),
+                    stop=(g == 1),
+                )
 
-        def yt_banks(j):
-            return ht_bank if j >= LATE and (j - LATE) % 2 == 0 else yt_bank
+        def z_affine(pair, s, on_vector=False):
+            if s == 0:
+                z_tiles[pair] = ring.tile([P, 4, C, 256], F32, name="z", bufs=3, align_bytes=64)
+            src = give_bank(("est", pair, s))[:]
+            dst = z_tiles[pair][:, s].rearrange("p c i -> p (c i)")
+            scale, shift = gain32[:, s : s + 1], bias32[:, s : s + 1]
+            if on_vector:
+                nc.vector.tensor_scalar(out=dst, in0=src, scalar1=scale, scalar2=shift, op0=ALU.mult, op1=ALU.add)
+            else:
+                nc.scalar.activation(out=dst, in_=src, func=ACT.Identity, scale=scale, bias=shift)
 
-        def est_matmul(j, half):
-            for s in range(2 * half, 2 * half + 2):
-                for g in range(2):
-                    nc.tensor.matmul_mx(
-                        out=est_banks(j)[s // 2][:, 256 * (s % 2) : 256 * (s % 2 + 1)],
-                        lhsT=basis_codes[:, g, P * s : P * (s + 1)].bitcast(FP8X4),
-                        lhsT_scale=basis_scale[:, g, P * s : P * (s + 1)],
-                        rhs=h_codes[:, j, 256 * g : 256 * (g + 1)].bitcast(FP8X4),
-                        rhs_scale=h_scale[:, j, 256 * g : 256 * (g + 1)],
-                        start=(g == 0),
-                        stop=(g == 1),
-                    )
-
-        def z_affine(j, half, on_vector=False):
-            if half == 0:
-                z_tiles[j] = ring.tile([P, 4, 256], F32, name="z", bufs=5, align_bytes=64)
-            for s in range(2 * half, 2 * half + 2):
-                src = est_banks(j)[s // 2][:, 256 * (s % 2) : 256 * (s % 2 + 1)]
-                scale, shift = gain32[:, s : s + 1], bias32[:, s : s + 1]
-                if on_vector:
-                    nc.vector.tensor_scalar(
-                        out=z_tiles[j][:, s], in0=src, scalar1=scale, scalar2=shift, op0=ALU.mult, op1=ALU.add
-                    )
-                else:
-                    nc.scalar.activation(out=z_tiles[j][:, s], in_=src, func=ACT.Identity, scale=scale, bias=shift)
-
-        def y_round(j, c, on_vector):
-            if c == 0:
-                yb_tiles[j] = ring.tile([P, C, 512], BF16, name="y_b", bufs=4, align_bytes=64)
-            lev = level_all[:, P * j : P * (j + 1)]
-            dst, src = yb_tiles[j][:, c], z_tiles[j][:, :, P * c : P * (c + 1)]
+        def y_round(n, lo, hi, on_vector):
+            if lo == 0:
+                yb_tiles[n] = ring.tile([P, 2, 512], BF16, name="y_b", bufs=4, align_bytes=64)
+            first, count = 256 * (n // 2) + P * lo, P * (hi - lo)
+            lev = level_all[:, first : first + count]
+            dst = yb_tiles[n][:, lo:hi].rearrange("p h k -> p (h k)")
+            src = z_tiles[n // 2][:, :, n % 2][:, :, P * lo : P * hi]
             if on_vector:
                 nc.vector.tensor_tensor(
                     out=dst.rearrange("p (a i s) -> p a s i", i=2, s=4),
                     in0=src.rearrange("p s (a i) -> p a s i", i=2),
-                    in1=lev.rearrange("p (a i) -> p a i", i=2).unsqueeze(2).broadcast_to([P, P // 2, 4, 2]),
+                    in1=lev.rearrange("p (a i) -> p a i", i=2).unsqueeze(2).broadcast_to([P, count // 2, 4, 2]),
                     op=ALU.mult,
                 )
             else:
                 nc.gpsimd.tensor_tensor(
                     out=dst.rearrange("p (i s) -> p i s", s=4),
                     in0=src.rearrange("p s i -> p i s"),
-                    in1=lev.unsqueeze(2).broadcast_to([P, P, 4]),
+                    in1=lev.unsqueeze(2).broadcast_to([P, count, 4]),
                     op=ALU.mult,
                 )
 
-        def y_quantize(j, c):
-            for c in (c,):
-                cols = slice(T * c + P * j, T * c + P * (j + 1))
-                quantize(y_codes[:, cols], y_scale[:, cols], yb_tiles[j][:, c])
+        def y_quantize(n):
+            lo = T * (n % 2) + 256 * (n // 2)
+            quantize(y_codes[:, lo : lo + 256], y_scale[:, lo : lo + 256], yb_tiles[n][:].rearrange("p h k -> p (h k)"))
 
-        def y_transpose(j, c):
+        def y_transpose(n, half):
+            ps = take_bank(("y", n, half))
             for s in range(4):
-                nc.tensor.transpose(yt_banks(j)[c][:, P * s : P * (s + 1)], z_tiles[j][:, s, P * c : P * (c + 1)], ident32[:])
+                nc.tensor.transpose(ps[:, P * s : P * (s + 1)], z_tiles[n // 2][:, s, n % 2, P * half : P * (half + 1)], ident32[:])
 
-        def y_copy(j, c, on_vector=False):
-            if c == 0:
-                y_tiles[j] = ring.tile([P, C, L], F32, name="y_rows", align_bytes=64)
-            dst = y_tiles[j][:, c].rearrange("p (m s) -> p m s", s=4)
-            src = yt_banks(j)[c][:].rearrange("p (s m) -> p m s", s=4)
+        def y_copy(n, half, on_vector=False):
+            if half == 0:
+                y_tiles[n] = ring.tile([P, 2, L], F32, name="y_rows", align_bytes=64)
+            j = 2 * (n // 2) + half
+            dst = y_tiles[n][:, half].rearrange("p (m s) -> p m s", s=4)
+            src = give_bank(("y", n, half))[:].rearrange("p (s m) -> p m s", s=4)
             if on_vector:
                 nc.vector.tensor_scalar(out=dst, in0=src, scalar1=level_col[:, j : j + 1], scalar2=None, op0=ALU.mult)
             else:
                 nc.scalar.activation(out=dst, in_=src, func=ACT.Copy, scale=level_col[:, j : j + 1])
 
-        def store_y(j, lo, hi):
-            rows = out_0[lo:hi, P * j : P * (j + 1), :].rearrange("c i l -> i c l")
-            nc.sync.dma_start(out=rows, in_=y_tiles[j][:, lo:hi])
+        def store_y(n, lo, hi):
+            rows = out_0[n % 2, 256 * (n // 2) : 256 * (n // 2 + 1), :].rearrange("(h i) l -> i h l", h=2)
+            nc.sync.dma_start(out=rows[:, lo:hi], in_=y_tiles[n][:, lo:hi])
 
         def store_codes(lo, hi):
             src = y_codes[:].bitcast(I32).rearrange("p (c i) -> p c i", c=C)
-            nc.sync.dma_start(out=codes_dram[:, :, P * lo : P * hi], in_=src[:, :, P * lo : P * hi])
+            cols = slice(256 * lo, 256 * hi)
+            nc.sync.dma_start(out=codes_dram[:, :, cols], in_=src[:, :, cols])
 
         def store_scales(q, eng):
             eng.dma_start(
                 out=out_2[0, 4 * q : 4 * q + 4, :].bitcast(I32), in_=y_scale[32 * q : 32 * q + 4, :].bitcast(I32)
             )
 
-        load_enc(0)
-        nc.vector.memset(in_scales[:].bitcast(U32), 0)
-        nc.vector.memset(level_rows[:], 0.0)
-        load_atom_scales(0)
-        make_identity(nc, ident16[:])
-        load_x_scales(0)
-        load_atom_scales(1)
-        load_enc(1)
-        load_x_scales(1)
-        load_mix(0, 0)
-        load_x(0, 256)
-        nc.gpsimd.dma_start(out=level_rows[0:NT, :], in_=level.rearrange("(j p) -> j p", p=P))
-        make_identity(nc, ident32[:])
-        nc.gpsimd.dma_start(out=gain_raw[:], in_=gain.rearrange("(p s) -> p s", s=4))
-        enc_interleave(False, 0, 1)
-        enc_interleave(True, 0, 0)
-        load_x_scales(2)
-        load_mask(0)
-        load_x_scales(3)
         load_mix(0, 1)
-        enc_interleave(False, 0, 0)
-        enc_interleave(True, 0, 1)
+        nc.vector.memset(in_scales[:].bitcast(U32), 0)
+        load_x_scales(0)
+        nc.vector.memset(level_rows[:], 0.0)
+        load_x_scales(1)
+        make_identity(nc, ident16[:])
+        load_enc(0)
+        enc_interleave(True, 0)
+        nc.gpsimd.dma_start(out=level_rows[0:NT, :], in_=level.rearrange("(j p) -> j p", p=P))
+        enc_interleave(False, 0)
+        load_x_scales(3)
+        load_mix(0, 0)
         enc_quantize(0, 0)
-        enc_interleave(False, 1, 0)
-        enc_interleave(True, 1, 1)
-        load_mask(1)
-        load_x(256, 1024)
-        enc_interleave(False, 1, 1)
-        enc_interleave(True, 1, 0)
-        spread_level()
-        enc_quantize(0, 1)
-        load_mask(2)
-        enc_quantize(1, 0)
-        load_atoms()
-        enc_quantize(1, 1)
-        load_atom_scales(2)
-        nc.gpsimd.dma_start(out=bias_raw[:], in_=bias.rearrange("(p s) -> p s", s=4))
-        w_matmul(0, 0)
-        load_atom_scales(3)
-        load_mask(3)
-        w_matmul(0, 1)
-        h_multiply(0, 0, 0)
-        mix_transpose(0, 0)
-        h_multiply(0, 0, 1)
-        load_mix(1, 0)
-        mix_transpose(0, 1)
-        mix_copy(0, 0, False)
-        h_multiply(0, 1, 0)
+        make_identity(nc, ident32[:])
         mix_transpose(0, 2)
-        mix_copy(0, 1, False)
-        h_multiply(0, 1, 1)
-        load_mix(1, 1)
-        w_matmul(1, 0)
-        nc.scalar.activation(out=gain32[:], in_=gain_raw[:], func=ACT.Identity)
-        mix_copy(0, 2, False)
-        w_matmul(1, 1)
-        h_multiply(1, 0, 0)
-        h_transpose(0, 0)
-        load_mask(4)
-        h_multiply(1, 0, 1)
+        mix_copy(0, 2, True)
         mix_transpose(0, 3)
-        h_copy(0, 0, False)
-        h_multiply(1, 1, 0)
-        h_transpose(0, 1)
+        enc_quantize(0, 1)
         mix_copy(0, 3, False)
-        load_mask(5)
-        h_multiply(1, 1, 1)
-        w_matmul(2, 0)
-        h_copy(0, 1, False)
-        load_mask(6)
-        h_transpose(1, 0)
-        mix_quantize(0, 0)
-        load_mask(7)
-        h_transpose(1, 1)
-        h_copy(1, 0, False)
-        mix_quantize(0, 1)
-        w_matmul(2, 1)
-        basis_matmul(0, 0)
-        h_multiply(2, 0, 0)
-        h_multiply(2, 0, 1)
-        basis_matmul(0, 1)
-        basis_copy(0, 0, False)
-        h_multiply(2, 1, 0)
-        basis_matmul(0, 2)
-        h_copy(1, 1, False)
-        h_multiply(2, 1, 1)
-        basis_copy(0, 1, False)
-        w_matmul(3, 0)
-        basis_matmul(0, 3)
-        h_quantize(0)
-        basis_copy(0, 2, False)
-        w_matmul(3, 1)
-        h_multiply(3, 0, 0)
-        basis_copy(0, 3, False)
+        level_transpose()
+        level_columns()
+        mix_transpose(0, 0)
+        load_x_scales(2)
+        mix_transpose(0, 1)
+        load_enc(1)
+        enc_interleave(False, 1)
+        enc_interleave(True, 1)
+        load_mix(1, 0)
         mix_transpose(1, 0)
-        h_multiply(3, 0, 1)
+        mix_copy(0, 0, True)
+        load_x(0, 256)
+        enc_quantize(1, 0)
+        enc_quantize(1, 1)
+        mix_copy(0, 1, False)
+        mix_quantize(0, 0)
+        load_atom_scales(1)
+        load_mask(0)
+        w_matmul(0, 0)
+        load_mix(1, 1)
+        mix_quantize(0, 1)
+        h_multiply(0, 0)
+        w_matmul(0, 1)
+        h_multiply(0, 1)
+        w_matmul(1, 0)
+        nc.gpsimd.dma_start(out=gain_raw[:], in_=gain.rearrange("(p s) -> p s", s=4))
         mix_transpose(1, 1)
+        load_mask(1)
+        load_atom_scales(2)
+        load_x(256, 1024)
         mix_copy(1, 0, False)
-        basis_quantize(0)
+        load_atoms()
+        nc.scalar.activation(out=gain32[:], in_=gain_raw[:], func=ACT.Identity)
         mix_transpose(1, 2)
         mix_copy(1, 1, False)
-        h_multiply(3, 1, 0)
-        mix_transpose(1, 3)
+        load_atom_scales(3)
+        w_matmul(1, 1)
+        load_atom_scales(0)
+        h_multiply(1, 0)
+        h_multiply(1, 1)
+        load_mask(2)
+        nc.gpsimd.dma_start(out=bias_raw[:], in_=bias.rearrange("(p s) -> p s", s=4))
+        load_mask(3)
         mix_copy(1, 2, False)
-        h_quantize(1)
-        h_transpose(2, 0)
+        load_mask(4)
+        w_matmul(2, 0)
+        w_matmul(2, 1)
+        load_mask(5)
+        basis_matmul(0, 2)
+        mix_transpose(1, 3)
+        basis_copy(0, 2, False)
+        h_transpose(0, 0)
+        h_transpose(0, 1)
+        h_transpose(1, 0)
+        h_multiply(2, 0)
+        h_transpose(1, 1)
         mix_copy(1, 3, False)
-        h_transpose(2, 1)
-        h_multiply(3, 1, 1)
-        w_matmul(4, 0)
-        h_copy(2, 0, False)
         mix_quantize(1, 0)
-        w_matmul(4, 1)
-        h_copy(2, 1, False)
-        h_transpose(3, 0)
+        load_mask(6)
+        w_matmul(3, 0)
+        h_copy(0, 0, False)
+        h_copy(0, 1, False)
+        h_copy(1, 0, False)
+        h_copy(1, 1, False)
+        basis_matmul(0, 1)
+        basis_matmul(0, 0)
+        basis_copy(0, 0, False)
         mix_quantize(1, 1)
-        nc.scalar.activation(out=bias32[:], in_=bias_raw[:], func=ACT.Identity)
-        basis_matmul(1, 0)
-        h_copy(3, 0, False)
-        h_multiply(4, 0, 0)
-        h_quantize(2)
-        basis_matmul(1, 1)
-        basis_copy(1, 0, False)
-        h_multiply(4, 0, 1)
         basis_matmul(1, 2)
-        basis_copy(1, 1, False)
-        h_multiply(4, 1, 0)
-        basis_matmul(1, 3)
         basis_copy(1, 2, False)
-        h_multiply(4, 1, 1)
-        w_matmul(5, 0)
+        w_matmul(3, 1)
+        h_multiply(2, 1)
+        w_matmul(4, 0)
+        basis_matmul(1, 1)
+        h_quantize(0, 1)
+        basis_matmul(1, 3)
+        h_multiply(3, 0)
+        basis_matmul(0, 3)
+        basis_matmul(1, 0)
+        nc.scalar.activation(out=bias32[:], in_=bias_raw[:], func=ACT.Identity)
+        basis_copy(0, 1, False)
+        basis_copy(1, 1, False)
+        h_multiply(3, 1)
+        h_quantize(0, 0)
         basis_copy(1, 3, False)
-        h_transpose(3, 1)
-        h_multiply(5, 0, 0)
-        h_transpose(4, 0)
-        h_copy(3, 1, False)
+        h_transpose(2, 0)
+        h_transpose(2, 1)
+        h_multiply(4, 0)
+        h_transpose(3, 0)
+        basis_copy(0, 3, False)
+        level_spread()
+        basis_copy(1, 0, False)
         basis_quantize(1)
+        basis_quantize(0)
+        h_transpose(3, 1)
+        w_matmul(4, 1)
+        h_copy(2, 0, False)
+        h_copy(2, 1, False)
+        w_matmul(5, 0)
         w_matmul(5, 1)
-        h_copy(4, 0, False)
+        h_copy(3, 0, False)
         est_matmul(0, 0)
-        h_quantize(3)
+        load_mask(7)
         est_matmul(0, 1)
-        h_multiply(5, 0, 1)
-        z_affine(0, 0, False)
-        h_transpose(4, 1)
-        h_multiply(5, 1, 0)
-        z_affine(0, 1, False)
-        est_matmul(1, 0)
-        h_multiply(5, 1, 1)
-        h_copy(4, 1, False)
-        est_matmul(1, 1)
-        y_round(0, 0, True)
-        z_affine(1, 0, False)
-        y_transpose(0, 0)
-        h_quantize(4)
-        z_affine(1, 1, False)
-        y_transpose(0, 1)
-        y_round(0, 1, True)
-        h_transpose(5, 0)
-        y_copy(0, 0, False)
+        h_multiply(4, 1)
+        level_copy()
+        est_matmul(0, 2)
         w_matmul(6, 0)
-        y_quantize(0, 0)
-        y_round(1, 0, True)
-        h_copy(5, 0, False)
-        est_matmul(2, 0)
-        y_quantize(0, 1)
-        y_round(1, 1, True)
+        est_matmul(0, 3)
+        z_affine(0, 0, False)
+        h_multiply(5, 0)
         w_matmul(6, 1)
-        z_affine(2, 0, False)
-        est_matmul(2, 1)
-        h_multiply(6, 0, 0)
-        y_copy(0, 1, False)
+        z_affine(0, 1, False)
+        h_transpose(4, 0)
+        z_affine(0, 2, False)
+        z_affine(0, 3, False)
+        h_multiply(5, 1)
+        h_multiply(6, 0)
+        h_copy(3, 1, False)
+        h_copy(4, 0, False)
+        h_transpose(4, 1)
+        h_copy(4, 1, False)
+        h_multiply(6, 1)
+        y_transpose(0, 0)
+        h_transpose(5, 0)
         h_transpose(5, 1)
-        h_multiply(6, 0, 1)
-        y_transpose(1, 0)
-        z_affine(2, 1, False)
-        store_y(0, 0, 2)
-        y_transpose(1, 1)
-        h_multiply(6, 1, 0)
-        est_matmul(3, 0)
-        y_copy(1, 0, False)
-        y_round(2, 0, True)
-        y_copy(1, 1, False)
-        est_matmul(3, 1)
-        y_round(2, 1, True)
-        z_affine(3, 0, False)
+        y_transpose(0, 1)
         w_matmul(7, 0)
-        h_multiply(6, 1, 1)
-        h_transpose(6, 0)
-        h_copy(5, 1, False)
-        y_transpose(2, 0)
-        y_quantize(1, 0)
-        y_quantize(1, 1)
-        y_transpose(2, 1)
-        y_quantize(2, 0)
-        h_copy(6, 0, False)
-        store_codes(0, 2)
-        h_multiply(7, 0, 0)
-        store_y(1, 0, 2)
+        h_copy(5, 0, False)
         w_matmul(7, 1)
-        z_affine(3, 1, False)
-        y_quantize(2, 1)
-        est_matmul(4, 0)
-        h_multiply(7, 0, 1)
-        y_copy(2, 0, False)
+        y_copy(0, 0, False)
+        y_transpose(1, 0)
+        h_copy(5, 1, False)
+        h_transpose(6, 0)
         h_transpose(6, 1)
-        h_quantize(5)
-        h_transpose(7, 0)
-        y_copy(2, 1, False)
-        y_round(3, 0, True)
-        y_transpose(3, 0)
+        y_copy(0, 1, False)
+        y_copy(1, 0, False)
+        h_quantize(1, 0)
+        h_quantize(1, 1)
+        est_matmul(1, 2)
+        est_matmul(1, 0)
+        z_affine(1, 0, False)
+        h_multiply(7, 0)
+        est_matmul(1, 3)
+        store_y(0, 0, 2)
+        h_copy(6, 0, False)
+        est_matmul(1, 1)
+        h_multiply(7, 1)
         h_copy(6, 1, False)
-        est_matmul(4, 1)
-        store_y(2, 0, 2)
-        h_multiply(7, 1, 0)
-        z_affine(4, 0, False)
-        y_transpose(3, 1)
-        h_multiply(7, 1, 1)
-        est_matmul(5, 0)
-        z_affine(4, 1, False)
-        y_quantize(3, 0)
-        h_quantize(6)
-        y_copy(3, 0, False)
-        est_matmul(5, 1)
-        z_affine(5, 0, True)
-        y_copy(3, 1, False)
+        h_quantize(2, 1)
+        h_quantize(2, 0)
+        y_transpose(1, 1)
+        z_affine(1, 1, False)
+        z_affine(1, 2, True)
+        y_round(0, 0, 2, True)
+        h_transpose(7, 0)
+        y_round(1, 0, 2, True)
         h_transpose(7, 1)
-        h_copy(7, 0, True)
-        y_transpose(4, 0)
-        z_affine(5, 1, False)
-        store_y(3, 0, 2)
-        y_transpose(4, 1)
-        y_round(3, 1, True)
-        est_matmul(6, 0)
-        y_copy(4, 0, False)
-        y_round(4, 0, True)
-        y_copy(4, 1, False)
-        est_matmul(6, 1)
-        y_round(4, 1, True)
-        y_transpose(5, 0)
+        z_affine(1, 3, False)
+        h_copy(7, 0, False)
         h_copy(7, 1, False)
-        y_quantize(3, 1)
-        y_quantize(4, 0)
-        store_codes(2, 4)
-        y_round(5, 0, True)
-        store_y(4, 0, 2)
-        z_affine(6, 0, False)
+        h_quantize(3, 1)
+        h_quantize(3, 0)
+        y_copy(1, 1, False)
+        est_matmul(2, 0)
+        est_matmul(2, 1)
+        y_transpose(2, 1)
+        store_y(1, 0, 2)
+        y_round(2, 0, 2, True)
+        y_transpose(3, 1)
+        z_affine(2, 0, False)
+        z_affine(2, 1, False)
+        y_transpose(2, 0)
+        y_copy(2, 0, False)
+        y_copy(2, 1, True)
+        est_matmul(2, 2)
+        y_quantize(0)
+        est_matmul(2, 3)
+        z_affine(2, 2, False)
+        z_affine(2, 3, False)
+        est_matmul(3, 2)
+        y_transpose(3, 0)
+        y_copy(3, 0, False)
+        est_matmul(3, 1)
+        y_round(3, 0, 2, True)
+        y_quantize(1)
+        y_copy(3, 1, False)
+        y_transpose(4, 0)
+        y_quantize(2)
+        y_transpose(4, 1)
+        y_copy(4, 0, False)
+        store_y(2, 0, 2)
+        y_copy(4, 1, False)
+        y_quantize(3)
+        est_matmul(3, 0)
+        y_transpose(5, 0)
         y_transpose(5, 1)
-        y_round(5, 1, True)
-        z_affine(6, 1, False)
+        y_round(4, 0, 2, True)
+        y_round(5, 0, 2, True)
+        z_affine(3, 0, False)
+        store_y(3, 0, 2)
+        store_y(4, 0, 2)
+        y_quantize(4)
+        est_matmul(3, 3)
+        store_codes(0, 2)
+        z_affine(3, 1, False)
+        y_quantize(5)
+        store_codes(2, 3)
+        z_affine(3, 2, False)
+        z_affine(3, 3, False)
         y_transpose(6, 0)
-        y_quantize(4, 1)
-        y_quantize(5, 0)
-        y_copy(5, 0, False)
-        y_quantize(5, 1)
         y_transpose(6, 1)
-        h_quantize(7)
-        store_codes(4, 6)
-        y_copy(5, 1, False)
-        y_round(6, 0, True)
-        est_matmul(7, 0)
+        y_copy(5, 0, False)
+        y_copy(5, 1, True)
         y_copy(6, 0, False)
         store_y(5, 0, 2)
-        y_round(6, 1, True)
-        est_matmul(7, 1)
-        y_copy(6, 1, False)
-        y_quantize(6, 0)
-        y_quantize(6, 1)
-        z_affine(7, 0, False)
-        z_affine(7, 1, True)
-        store_codes(6, 7)
-        store_y(6, 0, 2)
         y_transpose(7, 0)
-        y_round(7, 0, True)
-        y_transpose(7, 1)
+        y_round(6, 0, 2, True)
+        y_quantize(6)
+        y_copy(6, 1, False)
+        store_y(6, 0, 2)
         y_copy(7, 0, False)
-        y_round(7, 1, True)
-        y_copy(7, 1, False)
+        y_transpose(7, 1)
+        y_round(7, 0, 2, True)
+        y_quantize(7)
         store_y(7, 0, 1)
-        y_quantize(7, 0)
-        y_quantize(7, 1)
+        y_copy(7, 1, False)
         store_y(7, 1, 2)
-        store_codes(7, 8)
-        store_scales(3, nc.scalar)
+        store_codes(3, 4)
         store_scales(1, nc.scalar)
         store_scales(2, nc.sync)
         store_scales(0, nc.sync)
+        store_scales(3, nc.scalar)

@@ -18,8 +18,9 @@ ACT = mybir.ActivationFunctionType
 
 P = 128
 NT = T // P
-ENC_SPLIT = 80
+ENC_SPLIT = 0
 NUM_BANKS = 8
+ON_GPSIMD = ()
 
 
 def tile_masked_frame_decode_k4_kernel(
@@ -54,30 +55,30 @@ def tile_masked_frame_decode_k4_kernel(
         atom_scale = in_scales[:, T : T + 2 * L].rearrange("p (g n) -> p g n", g=2)
         x_codes = kept("x_codes", [P, T], U32)
         atom_codes = kept("atom_codes", [P, 2, 2 * L], U8)
-        enc_raw = kept("enc_raw", [P, 4, F], BF16)
-        enc_b = kept("enc_b", [P, 2, 256, 2, 4], BF16)
+        enc_raw = [kept("enc_raw%d" % g, [P, 4, 512], BF16) for g in range(2)]
+        enc_b = kept("enc_b", [P, 2, 2, 128, 2, 4], BF16)
         enc_codes = kept("enc_codes", [P, F], U32)
         enc_scale = kept("enc_scale", [P, F], U8)
         mask_sb = kept("mask_sb", [P, NT, C, F], BF16)
         mix_raw = kept("mix_raw", [P, 2, 4, R], BF16)
-        mix_b = kept("mix_b", [P, 2, 2, 2048], BF16)
-        mix_codes = kept("mix_codes", [P, 2, 2, 512], U32)
-        mix_scale = kept("mix_scale", [P, 2, 2, 512], U8)
+        mix_b = kept("mix_b", [P, 2, 4, 1024], BF16)
+        mix_codes = kept("mix_codes", [P, 2, 4, 256], U32)
+        mix_scale = kept("mix_scale", [P, 2, 4, 256], U8)
         basis_b = kept("basis_b", [P, 2, 2048], BF16)
         basis_codes = kept("basis_codes", [P, 2, 512], U32)
         basis_scale = kept("basis_scale", [P, 2, 512], U8)
         h_codes = kept("h_codes", [P, NT, 512], U32)
         h_scale = kept("h_scale", [P, NT, 512], U8)
-        y_codes = kept("y_codes", [P, C * T], U32)
+        y_codes = kept("y_codes", [P, NT, 256], U32)
         y_scale = kept("y_scale", [P, C * T], U8)
         gain_raw = kept("gain_raw", [P, 4], BF16)
         bias_raw = kept("bias_raw", [P, 4], BF16)
         gain32 = kept("gain32", [P, 4], F32)
         bias32 = kept("bias32", [P, 4], F32)
         level_rows = kept("level_rows", [P, P], BF16)
-        level_col16 = kept("level_col16", [P, NT], BF16)
         level_col = kept("level_col", [P, NT], F32)
-        level_all = kept("level_all", [P, T], F32)
+        level_all = kept("level_all", [P, T], BF16)
+        w_tiles = {}
         h_tiles, ht_tiles, z_tiles, yb_tiles, y_tiles = {}, {}, {}, {}, {}
 
         x_dram = x_words[0].rearrange("p n t -> p (n t)").bitcast(I32)
@@ -85,7 +86,7 @@ def tile_masked_frame_decode_k4_kernel(
 
         def load_enc(g):
             cols = slice(512 * g, 512 * (g + 1))
-            nc.sync.dma_start(out=enc_raw[:, :, cols], in_=enc[:, cols].rearrange("(p j) f -> p j f", j=4))
+            nc.sync.dma_start(out=enc_raw[g][:], in_=enc[:, cols].rearrange("(p j) f -> p j f", j=4))
 
         def load_x(lo, hi):
             nc.sync.dma_start(out=x_codes[:, lo:hi].bitcast(I32), in_=x_dram[:, lo:hi])
@@ -122,31 +123,21 @@ def tile_masked_frame_decode_k4_kernel(
 
         def level_columns():
             col_ps = give_bank("level_col")[:].bitcast(BF16)[:, 0:NT]
-            nc.scalar.copy(out=level_col16[:], in_=col_ps)
             nc.scalar.activation(out=level_col[:], in_=col_ps, func=ACT.Identity)
 
-        def level_spread():
-            all_ps = take_bank("level_all")[:].bitcast(BF16)
-            for j in range(NT):
-                nc.tensor.transpose(
-                    all_ps[:, P * j : P * (j + 1)], level_col16[:, j : j + 1].to_broadcast([P, P]), ident16[:]
-                )
+        def load_level_all():
+            nc.sync.dma_start(out=level_all[:], in_=level.partition_broadcast(P))
 
-        def level_copy():
-            nc.scalar.copy(out=level_all[:], in_=give_bank("level_all")[:].bitcast(BF16))
-
-        def enc_interleave(on_vector, g):
-            lo, hi = (128 * g, 128 * g + ENC_SPLIT) if on_vector else (128 * g + ENC_SPLIT, 128 * (g + 1))
-            src = enc_raw[:].rearrange("p j (m u e) -> p m j u e", u=2, e=2)[:, lo:hi]
-            dst = enc_b[:, :, lo:hi].rearrange("p u m e j -> p m j u e")
-            copy_on(on_vector, dst, src)
+        def enc_interleave(g, u, lo, hi, on_vector):
+            src = enc_raw[g][:].rearrange("p j (m u e) -> p u m j e", u=2, e=2)[:, u, lo:hi]
+            copy_on(on_vector, enc_b[:, g, u, lo:hi].rearrange("p m e j -> p m j e"), src)
 
         def quantize(codes, scales, values):
             nc.vector.quantize_mx(out=codes.bitcast(FP8X4), scales=scales, in_=values)
 
         def enc_quantize(g, u):
             cols = slice(512 * u + 256 * g, 512 * u + 256 * (g + 1))
-            values = enc_b[:, u, 128 * g : 128 * (g + 1)].rearrange("p m e j -> p (m e j)")
+            values = enc_b[:, g, u].rearrange("p m e j -> p (m e j)")
             quantize(enc_codes[:, cols], enc_scale[:, cols], values)
 
         def mix_transpose(g, t):
@@ -158,11 +149,16 @@ def tile_masked_frame_decode_k4_kernel(
                     nc.tensor.transpose(ps[:, P * n : P * (n + 1)], words[:, 256 * kg + u : 256 * (kg + 1) : 2], ident32[:])
 
         def mix_copy(g, t, on_vector=False):
-            dst = mix_b[:, g].bitcast(F32).rearrange("p k (t f u) -> p t k f u", t=4, u=2)[:, t]
+            dst = mix_b[:, g, t].bitcast(F32).rearrange("p (k f u) -> p k f u", k=2, u=2)
             copy_on(on_vector, dst, give_bank(("mix", g, t))[:].rearrange("p (k u f) -> p k f u", k=2, u=2))
 
-        def mix_quantize(g, kg):
-            quantize(mix_codes[:, g, kg], mix_scale[:, g, kg], mix_b[:, g, kg])
+        def mix_quantize(g, half):
+            slots = slice(2 * half, 2 * half + 2)
+            quantize(
+                mix_codes[:, g, slots].rearrange("p t n -> p (t n)"),
+                mix_scale[:, g, slots].rearrange("p t n -> p (t n)"),
+                mix_b[:, g, slots].rearrange("p t n -> p (t n)"),
+            )
 
         def basis_matmul(g, lq):
             ps = take_bank(("basis", g, lq))
@@ -170,8 +166,8 @@ def tile_masked_frame_decode_k4_kernel(
                 for kg in range(2):
                     nc.tensor.matmul_mx(
                         out=ps[:, P * t : P * (t + 1)],
-                        lhsT=mix_codes[:, g, kg, P * t : P * (t + 1)].bitcast(FP8X4),
-                        lhsT_scale=mix_scale[:, g, kg, P * t : P * (t + 1)],
+                        lhsT=mix_codes[:, g, t, P * kg : P * (kg + 1)].bitcast(FP8X4),
+                        lhsT_scale=mix_scale[:, g, t, P * kg : P * (kg + 1)],
                         rhs=atom_codes[:, kg, 256 * lq : 256 * (lq + 1)].bitcast(FP4X4),
                         rhs_scale=atom_scale[:, kg, P * lq : P * (lq + 1)],
                         start=(kg == 0),
@@ -198,35 +194,53 @@ def tile_masked_frame_decode_k4_kernel(
                 stop=True,
             )
 
-        def h_multiply(j, u):
+        def h_tile(j, u):
             if u == 0:
                 h_tiles[j] = ring.tile([P, 2, C, 512], BF16, name="h_rows", align_bytes=64)
-            nc.vector.scalar_tensor_tensor(
-                out=h_tiles[j][:, u].rearrange("p c (m e) -> p c m e", e=2),
-                in0=give_bank(("w", j, u))[:].rearrange("p (m e) -> p m e", e=2).unsqueeze(1).broadcast_to([P, C, 256, 2]),
-                scalar=0.0,
-                in1=mask_sb[:, j].rearrange("p c (m u e) -> p u c m e", u=2, e=2)[:, u],
-                op0=ALU.max,
-                op1=ALU.mult,
-            )
+            return h_tiles[j][:, u].rearrange("p c (m e) -> p c m e", e=2)
 
-        def h_transpose(j, c):
-            ps = take_bank(("h", j, c))
-            for g in range(2):
+        def both_sources(w_half):
+            return w_half.rearrange("p (m e) -> p m e", e=2).unsqueeze(1).broadcast_to([P, C, 256, 2])
+
+        def mask_half(j, u):
+            return mask_sb[:, j].rearrange("p c (m u e) -> p u c m e", u=2, e=2)[:, u]
+
+        def w_relu(j, u):
+            w_tiles[j, u] = ring.tile([P, 512], F32, name="w_sb", bufs=2, align_bytes=64)
+            nc.scalar.activation(out=w_tiles[j, u][:], in_=give_bank(("w", j, u))[:], func=ACT.Relu)
+
+        def h_multiply(j, u):
+            if (j, u) in ON_GPSIMD:
+                nc.gpsimd.tensor_tensor(
+                    out=h_tile(j, u), in0=both_sources(w_tiles[j, u][:]), in1=mask_half(j, u), op=ALU.mult
+                )
+            else:
+                nc.vector.scalar_tensor_tensor(
+                    out=h_tile(j, u),
+                    in0=both_sources(give_bank(("w", j, u))[:]),
+                    scalar=0.0,
+                    in1=mask_half(j, u),
+                    op0=ALU.max,
+                    op1=ALU.mult,
+                )
+
+        def h_transpose(j, g):
+            ps = take_bank(("h", j, g))
+            for c in range(C):
                 for u in range(2):
-                    n = 2 * g + u
+                    n = 2 * c + u
                     words = h_tiles[j][:, u, c].bitcast(F32)
                     nc.tensor.transpose(ps[:, P * n : P * (n + 1)], words[:, P * g : P * (g + 1)], ident32[:])
 
-        def h_copy(j, c, on_vector=False):
+        def h_copy(j, g, on_vector=False):
             pair, half = j // 2, j % 2
-            if half == 0 and c == 0:
-                ht_tiles[pair] = ring.tile([P, 2, 2048], BF16, name="h_cols", bufs=2, align_bytes=64)
-            dst = ht_tiles[pair][:].bitcast(F32).rearrange("p g (c h i u) -> p c h g i u", c=C, h=2, u=2)[:, c, half]
-            copy_on(on_vector, dst, give_bank(("h", j, c))[:].rearrange("p (g u i) -> p g i u", g=2, u=2))
+            if half == 0:
+                ht_tiles[pair, g] = ring.tile([P, 2048], BF16, name="h_cols", bufs=4, align_bytes=64)
+            dst = ht_tiles[pair, g][:].bitcast(F32).rearrange("p (c h i u) -> p h c i u", c=C, h=2, u=2)[:, half]
+            copy_on(on_vector, dst, give_bank(("h", j, g))[:].rearrange("p (c u i) -> p c i u", c=C, u=2))
 
         def h_quantize(pair, g):
-            quantize(h_codes[:, 2 * pair + g], h_scale[:, 2 * pair + g], ht_tiles[pair][:, g])
+            quantize(h_codes[:, 2 * pair + g], h_scale[:, 2 * pair + g], ht_tiles[pair, g][:])
 
         def est_matmul(pair, s):
             ps = take_bank(("est", pair, s))
@@ -276,7 +290,7 @@ def tile_masked_frame_decode_k4_kernel(
 
         def y_quantize(n):
             lo = T * (n % 2) + 256 * (n // 2)
-            quantize(y_codes[:, lo : lo + 256], y_scale[:, lo : lo + 256], yb_tiles[n][:].rearrange("p h k -> p (h k)"))
+            quantize(y_codes[:, n], y_scale[:, lo : lo + 256], yb_tiles[n][:].rearrange("p h k -> p (h k)"))
 
         def y_transpose(n, half):
             ps = take_bank(("y", n, half))
@@ -298,265 +312,285 @@ def tile_masked_frame_decode_k4_kernel(
             rows = out_0[n % 2, 256 * (n // 2) : 256 * (n // 2 + 1), :].rearrange("(h i) l -> i h l", h=2)
             nc.sync.dma_start(out=rows[:, lo:hi], in_=y_tiles[n][:, lo:hi])
 
-        def store_codes(lo, hi):
-            src = y_codes[:].bitcast(I32).rearrange("p (c i) -> p c i", c=C)
-            cols = slice(256 * lo, 256 * hi)
-            nc.sync.dma_start(out=codes_dram[:, :, cols], in_=src[:, :, cols])
+        def store_codes(pair, lo, hi):
+            nc.sync.dma_start(
+                out=codes_dram[:, lo:hi, 256 * pair : 256 * (pair + 1)],
+                in_=y_codes[:, 2 * pair + lo : 2 * pair + hi].bitcast(I32),
+            )
+
+        def ident_cast():
+            nc.scalar.activation(out=ident16[:], in_=ident32[:], func=ACT.Identity)
+
+        def warm_up(first):
+            ps = take_bank("warm")
+            for n in range(first, first + 2):
+                nc.tensor.matmul_mx(
+                    out=ps[:, 256 * (n % 2) : 256 * (n % 2 + 1)],
+                    lhsT=enc_codes[:, 0:P].bitcast(FP8X4),
+                    lhsT_scale=enc_scale[:, 0:P],
+                    rhs=enc_codes[:, 0:256].bitcast(FP8X4),
+                    rhs_scale=enc_scale[:, 0:256],
+                    start=True,
+                    stop=True,
+                )
+            give_bank("warm")
 
         def store_scales(q, eng):
             eng.dma_start(
                 out=out_2[0, 4 * q : 4 * q + 4, :].bitcast(I32), in_=y_scale[32 * q : 32 * q + 4, :].bitcast(I32)
             )
 
-        load_mix(0, 1)
         nc.vector.memset(in_scales[:].bitcast(U32), 0)
-        load_x_scales(0)
         nc.vector.memset(level_rows[:], 0.0)
-        load_x_scales(1)
-        make_identity(nc, ident16[:])
         load_enc(0)
-        enc_interleave(True, 0)
-        nc.gpsimd.dma_start(out=level_rows[0:NT, :], in_=level.rearrange("(j p) -> j p", p=P))
-        enc_interleave(False, 0)
-        load_x_scales(3)
-        load_mix(0, 0)
-        enc_quantize(0, 0)
         make_identity(nc, ident32[:])
-        mix_transpose(0, 2)
-        mix_copy(0, 2, True)
-        mix_transpose(0, 3)
-        enc_quantize(0, 1)
-        mix_copy(0, 3, False)
-        level_transpose()
-        level_columns()
-        mix_transpose(0, 0)
-        load_x_scales(2)
-        mix_transpose(0, 1)
         load_enc(1)
-        enc_interleave(False, 1)
-        enc_interleave(True, 1)
-        load_mix(1, 0)
-        mix_transpose(1, 0)
-        mix_copy(0, 0, True)
-        load_x(0, 256)
-        enc_quantize(1, 0)
-        enc_quantize(1, 1)
-        mix_copy(0, 1, False)
-        mix_quantize(0, 0)
-        load_atom_scales(1)
-        load_mask(0)
-        w_matmul(0, 0)
-        load_mix(1, 1)
-        mix_quantize(0, 1)
-        h_multiply(0, 0)
-        w_matmul(0, 1)
-        h_multiply(0, 1)
-        w_matmul(1, 0)
+        nc.gpsimd.dma_start(out=level_rows[0:NT, :], in_=level.rearrange("(j p) -> j p", p=P))
+        enc_interleave(0, 0, 0, 128, True)
         nc.gpsimd.dma_start(out=gain_raw[:], in_=gain.rearrange("(p s) -> p s", s=4))
-        mix_transpose(1, 1)
+        enc_quantize(0, 0)
+        warm_up(0)
+        load_x_scales(1)
+        enc_interleave(1, 0, 0, 128, True)
+        ident_cast()
+        enc_interleave(0, 1, 0, 128, False)
+        enc_quantize(0, 1)
+        enc_quantize(1, 0)
+        load_x_scales(0)
+        load_x_scales(3)
+        warm_up(2)
+        load_x_scales(2)
+        load_x(0, 256)
+        w_matmul(0, 0)
+        load_mask(0)
+        load_mix(0, 1)
+        enc_interleave(1, 1, 0, 128, False)
+        enc_quantize(1, 1)
+        w_matmul(0, 1)
+        w_matmul(1, 0)
         load_mask(1)
-        load_atom_scales(2)
-        load_x(256, 1024)
-        mix_copy(1, 0, False)
-        load_atoms()
-        nc.scalar.activation(out=gain32[:], in_=gain_raw[:], func=ACT.Identity)
-        mix_transpose(1, 2)
-        mix_copy(1, 1, False)
-        load_atom_scales(3)
         w_matmul(1, 1)
-        load_atom_scales(0)
+        h_multiply(0, 0)
+        load_x(256, 1024)
+        load_mix(1, 0)
+        mix_transpose(0, 3)
+        mix_transpose(0, 2)
+        mix_copy(0, 3, False)
+        h_multiply(0, 1)
+        load_atom_scales(3)
+        h_transpose(0, 0)
         h_multiply(1, 0)
-        h_multiply(1, 1)
+        load_atom_scales(1)
+        load_atom_scales(0)
+        mix_copy(0, 2, False)
         load_mask(2)
-        nc.gpsimd.dma_start(out=bias_raw[:], in_=bias.rearrange("(p s) -> p s", s=4))
-        load_mask(3)
-        mix_copy(1, 2, False)
-        load_mask(4)
         w_matmul(2, 0)
         w_matmul(2, 1)
-        load_mask(5)
-        basis_matmul(0, 2)
-        mix_transpose(1, 3)
-        basis_copy(0, 2, False)
-        h_transpose(0, 0)
+        level_transpose()
+        level_columns()
+        load_mix(0, 0)
         h_transpose(0, 1)
-        h_transpose(1, 0)
-        h_multiply(2, 0)
-        h_transpose(1, 1)
-        mix_copy(1, 3, False)
-        mix_quantize(1, 0)
-        load_mask(6)
-        w_matmul(3, 0)
+        h_multiply(1, 1)
         h_copy(0, 0, False)
         h_copy(0, 1, False)
+        mix_transpose(1, 0)
+        h_transpose(1, 0)
+        mix_transpose(1, 1)
+        w_matmul(3, 0)
+        w_matmul(3, 1)
+        h_transpose(1, 1)
+        mix_copy(1, 0, False)
+        mix_quantize(0, 1)
+        mix_copy(1, 1, False)
+        mix_transpose(0, 0)
         h_copy(1, 0, False)
         h_copy(1, 1, False)
-        basis_matmul(0, 1)
-        basis_matmul(0, 0)
-        basis_copy(0, 0, False)
-        mix_quantize(1, 1)
-        basis_matmul(1, 2)
-        basis_copy(1, 2, False)
-        w_matmul(3, 1)
+        load_atom_scales(2)
+        mix_transpose(0, 1)
+        h_multiply(2, 0)
+        nc.gpsimd.dma_start(out=bias_raw[:], in_=bias.rearrange("(p s) -> p s", s=4))
+        load_mask(3)
         h_multiply(2, 1)
-        w_matmul(4, 0)
-        basis_matmul(1, 1)
-        h_quantize(0, 1)
-        basis_matmul(1, 3)
-        h_multiply(3, 0)
-        basis_matmul(0, 3)
-        basis_matmul(1, 0)
-        nc.scalar.activation(out=bias32[:], in_=bias_raw[:], func=ACT.Identity)
-        basis_copy(0, 1, False)
-        basis_copy(1, 1, False)
-        h_multiply(3, 1)
-        h_quantize(0, 0)
-        basis_copy(1, 3, False)
         h_transpose(2, 0)
         h_transpose(2, 1)
-        h_multiply(4, 0)
-        h_transpose(3, 0)
-        basis_copy(0, 3, False)
-        level_spread()
-        basis_copy(1, 0, False)
-        basis_quantize(1)
-        basis_quantize(0)
-        h_transpose(3, 1)
-        w_matmul(4, 1)
+        load_mix(1, 1)
+        mix_copy(0, 0, False)
+        mix_copy(0, 1, False)
+        load_atoms()
+        load_mask(4)
         h_copy(2, 0, False)
+        w_matmul(4, 0)
+        w_matmul(4, 1)
+        mix_transpose(1, 3)
         h_copy(2, 1, False)
-        w_matmul(5, 0)
-        w_matmul(5, 1)
+        mix_transpose(1, 2)
+        mix_copy(1, 3, False)
+        h_multiply(3, 0)
+        h_multiply(3, 1)
+        h_transpose(3, 0)
+        load_level_all()
+        load_mask(5)
+        mix_copy(1, 2, False)
+        h_transpose(3, 1)
         h_copy(3, 0, False)
-        est_matmul(0, 0)
-        load_mask(7)
-        est_matmul(0, 1)
-        h_multiply(4, 1)
-        level_copy()
-        est_matmul(0, 2)
-        w_matmul(6, 0)
-        est_matmul(0, 3)
-        z_affine(0, 0, False)
-        h_multiply(5, 0)
-        w_matmul(6, 1)
-        z_affine(0, 1, False)
-        h_transpose(4, 0)
-        z_affine(0, 2, False)
-        z_affine(0, 3, False)
-        h_multiply(5, 1)
-        h_multiply(6, 0)
         h_copy(3, 1, False)
-        h_copy(4, 0, False)
+        mix_quantize(0, 0)
+        basis_matmul(0, 0)
+        mix_quantize(1, 0)
+        h_quantize(0, 1)
+        basis_copy(0, 0, False)
+        nc.scalar.activation(out=gain32[:], in_=gain_raw[:], func=ACT.Identity)
+        basis_matmul(0, 1)
+        mix_quantize(1, 1)
+        basis_matmul(1, 0)
+        basis_copy(1, 0, False)
+        basis_copy(0, 1, False)
+        h_multiply(4, 0)
+        h_multiply(4, 1)
+        load_mask(6)
+        basis_matmul(1, 1)
+        w_matmul(5, 0)
+        basis_matmul(0, 2)
+        basis_copy(1, 1, False)
+        h_quantize(0, 0)
+        basis_copy(0, 2, False)
+        w_matmul(5, 1)
+        basis_matmul(1, 2)
+        basis_matmul(0, 3)
+        h_multiply(5, 0)
+        basis_copy(1, 2, False)
+        basis_matmul(1, 3)
+        h_transpose(4, 0)
         h_transpose(4, 1)
-        h_copy(4, 1, False)
-        h_multiply(6, 1)
-        y_transpose(0, 0)
+        h_multiply(5, 1)
         h_transpose(5, 0)
         h_transpose(5, 1)
-        y_transpose(0, 1)
-        w_matmul(7, 0)
+        nc.scalar.activation(out=bias32[:], in_=bias_raw[:], func=ACT.Identity)
+        basis_copy(0, 3, False)
+        basis_quantize(0)
+        basis_copy(1, 3, False)
+        h_copy(4, 0, False)
+        h_copy(4, 1, False)
+        load_mask(7)
         h_copy(5, 0, False)
-        w_matmul(7, 1)
-        y_copy(0, 0, False)
-        y_transpose(1, 0)
-        h_copy(5, 1, False)
-        h_transpose(6, 0)
-        h_transpose(6, 1)
-        y_copy(0, 1, False)
-        y_copy(1, 0, False)
+        w_matmul(6, 0)
+        basis_quantize(1)
+        est_matmul(0, 0)
         h_quantize(1, 0)
+        est_matmul(0, 1)
+        w_matmul(6, 1)
+        est_matmul(0, 2)
+        est_matmul(0, 3)
+        h_multiply(6, 0)
         h_quantize(1, 1)
-        est_matmul(1, 2)
-        est_matmul(1, 0)
-        z_affine(1, 0, False)
-        h_multiply(7, 0)
-        est_matmul(1, 3)
-        store_y(0, 0, 2)
-        h_copy(6, 0, False)
-        est_matmul(1, 1)
-        h_multiply(7, 1)
-        h_copy(6, 1, False)
+        h_copy(5, 1, False)
         h_quantize(2, 1)
-        h_quantize(2, 0)
-        y_transpose(1, 1)
+        z_affine(0, 0, False)
+        z_affine(0, 1, False)
+        z_affine(0, 2, False)
+        est_matmul(1, 1)
+        est_matmul(1, 0)
+        h_multiply(6, 1)
+        z_affine(0, 3, False)
+        y_transpose(0, 0)
+        z_affine(1, 0, False)
         z_affine(1, 1, False)
-        z_affine(1, 2, True)
+        y_transpose(0, 1)
         y_round(0, 0, 2, True)
-        h_transpose(7, 0)
-        y_round(1, 0, 2, True)
-        h_transpose(7, 1)
-        z_affine(1, 3, False)
-        h_copy(7, 0, False)
-        h_copy(7, 1, False)
-        h_quantize(3, 1)
-        h_quantize(3, 0)
+        y_transpose(1, 0)
+        est_matmul(1, 3)
+        est_matmul(1, 2)
+        y_transpose(1, 1)
+        h_transpose(6, 0)
+        y_copy(0, 0, False)
+        y_copy(0, 1, False)
+        z_affine(1, 2, False)
+        h_quantize(2, 0)
+        w_matmul(7, 0)
+        w_matmul(7, 1)
+        z_affine(1, 3, True)
+        y_transpose(2, 0)
+        y_transpose(3, 0)
+        y_copy(1, 0, False)
         y_copy(1, 1, False)
+        h_copy(6, 0, False)
+        y_round(1, 0, 2, True)
+        y_round(2, 0, 2, True)
+        h_multiply(7, 0)
+        h_multiply(7, 1)
+        y_copy(2, 0, False)
+        store_y(0, 0, 2)
+        y_transpose(2, 1)
+        h_transpose(6, 1)
+        y_copy(2, 1, False)
+        store_y(1, 0, 2)
+        h_copy(6, 1, False)
         est_matmul(2, 0)
         est_matmul(2, 1)
-        y_transpose(2, 1)
-        store_y(1, 0, 2)
-        y_round(2, 0, 2, True)
-        y_transpose(3, 1)
-        z_affine(2, 0, False)
-        z_affine(2, 1, False)
-        y_transpose(2, 0)
-        y_copy(2, 0, False)
-        y_copy(2, 1, True)
         est_matmul(2, 2)
-        y_quantize(0)
-        est_matmul(2, 3)
-        z_affine(2, 2, False)
-        z_affine(2, 3, False)
-        est_matmul(3, 2)
-        y_transpose(3, 0)
-        y_copy(3, 0, False)
-        est_matmul(3, 1)
-        y_round(3, 0, 2, True)
         y_quantize(1)
+        z_affine(2, 0, False)
+        h_transpose(7, 0)
+        z_affine(2, 1, False)
+        z_affine(2, 2, False)
+        y_round(3, 0, 2, True)
+        y_quantize(0)
+        y_quantize(3)
+        h_transpose(7, 1)
+        est_matmul(2, 3)
+        h_copy(7, 0, False)
+        h_copy(7, 1, True)
+        store_y(2, 0, 2)
+        store_codes(0, 0, 2)
+        h_quantize(3, 0)
+        z_affine(2, 3, False)
+        y_copy(3, 0, False)
+        y_transpose(3, 1)
         y_copy(3, 1, False)
+        store_y(3, 0, 2)
+        y_transpose(5, 0)
+        h_quantize(3, 1)
         y_transpose(4, 0)
         y_quantize(2)
+        store_codes(1, 0, 2)
         y_transpose(4, 1)
-        y_copy(4, 0, False)
-        store_y(2, 0, 2)
-        y_copy(4, 1, False)
-        y_quantize(3)
-        est_matmul(3, 0)
-        y_transpose(5, 0)
         y_transpose(5, 1)
+        y_copy(4, 0, False)
+        y_copy(4, 1, False)
         y_round(4, 0, 2, True)
-        y_round(5, 0, 2, True)
-        z_affine(3, 0, False)
-        store_y(3, 0, 2)
-        store_y(4, 0, 2)
-        y_quantize(4)
-        est_matmul(3, 3)
-        store_codes(0, 2)
-        z_affine(3, 1, False)
-        y_quantize(5)
-        store_codes(2, 3)
-        z_affine(3, 2, False)
-        z_affine(3, 3, False)
-        y_transpose(6, 0)
-        y_transpose(6, 1)
+        est_matmul(3, 1)
         y_copy(5, 0, False)
-        y_copy(5, 1, True)
-        y_copy(6, 0, False)
+        est_matmul(3, 0)
+        z_affine(3, 0, False)
+        z_affine(3, 1, True)
+        est_matmul(3, 2)
+        store_y(4, 0, 2)
+        est_matmul(3, 3)
+        z_affine(3, 2, True)
+        y_copy(5, 1, False)
+        y_round(5, 0, 2, True)
+        y_quantize(4)
+        z_affine(3, 3, False)
         store_y(5, 0, 2)
-        y_transpose(7, 0)
+        y_quantize(5)
+        y_transpose(6, 0)
         y_round(6, 0, 2, True)
-        y_quantize(6)
-        y_copy(6, 1, False)
-        store_y(6, 0, 2)
-        y_copy(7, 0, False)
-        y_transpose(7, 1)
         y_round(7, 0, 2, True)
-        y_quantize(7)
+        y_transpose(6, 1)
+        y_transpose(7, 0)
+        y_copy(6, 0, False)
+        y_copy(6, 1, False)
+        y_copy(7, 0, False)
+        store_codes(2, 0, 2)
+        store_y(6, 0, 2)
+        y_quantize(6)
         store_y(7, 0, 1)
+        y_transpose(7, 1)
+        y_quantize(7)
         y_copy(7, 1, False)
         store_y(7, 1, 2)
-        store_codes(3, 4)
         store_scales(1, nc.scalar)
         store_scales(2, nc.sync)
-        store_scales(0, nc.sync)
+        store_codes(3, 0, 2)
         store_scales(3, nc.scalar)
+        store_scales(0, nc.sync)

from contextlib import ExitStack

import concourse.mybir as mybir
from concourse.masks import make_identity

C, T, F, L, R = 2, 1024, 1024, 512, 1024
FLOPS = 2 * (T * F * L + F * L * R + C * T * L * F)

F32 = mybir.dt.float32
BF16 = mybir.dt.bfloat16
I32 = mybir.dt.int32
U32 = mybir.dt.uint32
U8 = mybir.dt.uint8
FP8X4 = mybir.dt.float8_e4m3fn_x4
FP4X4 = mybir.dt.float4_e2m1fn_x4
ALU = mybir.AluOpType
ACT = mybir.ActivationFunctionType

P = 128
NT = T // P
ENC_SPLIT = 0
NUM_BANKS = 8
ON_GPSIMD = ()


def tile_masked_frame_decode_k4_kernel(
    tc, x_words, x_scales, enc, mask, mix, atoms_words, atoms_scales, gain, bias, level, out_0, out_1, out_2
):
    nc = tc.nc
    with ExitStack() as ctx:
        keep = ctx.enter_context(tc.tile_pool(name="keep", bufs=1))
        ring = ctx.enter_context(tc.tile_pool(name="ring", bufs=3))
        psum = ctx.enter_context(tc.psum_pool(name="psum", bufs=1))
        ctx.enter_context(tc.manual_schedule())

        def kept(name, shape, dtype):
            return keep.tile(shape, dtype, name=name, align_bytes=64)

        free_banks = [psum.tile([P, 512], F32, name="bank%d" % i) for i in range(NUM_BANKS)]
        held = {}

        def take_bank(key):
            held[key] = free_banks[0]
            free_banks.remove(held[key])
            return held[key]

        def give_bank(key):
            free_banks.append(held[key])
            return held[key]

        ident32 = kept("ident32", [P, P], F32)
        ident16 = kept("ident16", [P, P], BF16)
        in_scales = kept("in_scales", [P, 2048], U8)
        x_scale = in_scales[:, 0:T]
        atom_scale = in_scales[:, T : T + 2 * L].rearrange("p (g n) -> p g n", g=2)
        x_codes = kept("x_codes", [P, T], U32)
        atom_codes = kept("atom_codes", [P, 2, 2 * L], U8)
        enc_raw = [kept("enc_raw%d" % g, [P, 4, 512], BF16) for g in range(2)]
        enc_b = kept("enc_b", [P, 2, 2, 128, 2, 4], BF16)
        enc_codes = kept("enc_codes", [P, F], U32)
        enc_scale = kept("enc_scale", [P, F], U8)
        mask_sb = kept("mask_sb", [P, NT, C, F], BF16)
        mix_raw = kept("mix_raw", [P, 2, 4, R], BF16)
        mix_b = kept("mix_b", [P, 2, 4, 1024], BF16)
        mix_codes = kept("mix_codes", [P, 2, 4, 256], U32)
        mix_scale = kept("mix_scale", [P, 2, 4, 256], U8)
        basis_b = kept("basis_b", [P, 2, 2048], BF16)
        basis_codes = kept("basis_codes", [P, 2, 512], U32)
        basis_scale = kept("basis_scale", [P, 2, 512], U8)
        h_codes = kept("h_codes", [P, NT, 512], U32)
        h_scale = kept("h_scale", [P, NT, 512], U8)
        y_codes = kept("y_codes", [P, NT, 256], U32)
        y_scale = kept("y_scale", [P, C * T], U8)
        gain_raw = kept("gain_raw", [P, 4], BF16)
        bias_raw = kept("bias_raw", [P, 4], BF16)
        gain32 = kept("gain32", [P, 4], F32)
        bias32 = kept("bias32", [P, 4], F32)
        level_rows = kept("level_rows", [P, P], BF16)
        level_col = kept("level_col", [P, NT], F32)
        level_all = kept("level_all", [P, T], BF16)
        w_tiles = {}
        h_tiles, ht_tiles, z_tiles, yb_tiles, y_tiles = {}, {}, {}, {}, {}

        x_dram = x_words[0].rearrange("p n t -> p (n t)").bitcast(I32)
        codes_dram = out_1[0].rearrange("p m t -> p (m t)").bitcast(I32).rearrange("p (c i) -> p c i", c=C)

        def load_enc(g):
            cols = slice(512 * g, 512 * (g + 1))
            nc.sync.dma_start(out=enc_raw[g][:], in_=enc[:, cols].rearrange("(p j) f -> p j f", j=4))

        def load_x(lo, hi):
            nc.sync.dma_start(out=x_codes[:, lo:hi].bitcast(I32), in_=x_dram[:, lo:hi])

        def load_mask(j):
            nc.sync.dma_start(out=mask_sb[:, j], in_=mask[:, P * j : P * (j + 1), :].rearrange("c i f -> i c f"))

        def load_mix(g, half):
            rows = mix[512 * g : 512 * (g + 1), :].rearrange("(m t) k -> m t k", t=4)
            nc.sync.dma_start(out=mix_raw[:, g, 2 * half : 2 * half + 2, :], in_=rows[:, 2 * half : 2 * half + 2, :])

        def load_atoms():
            nc.sync.dma_start(out=atom_codes[:].bitcast(I32), in_=atoms_words.rearrange("g p n -> p g n").bitcast(I32))

        def load_x_scales(q):
            nc.sync.dma_start(
                out=x_scale[32 * q : 32 * q + 4, :].bitcast(I32), in_=x_scales[0, 4 * q : 4 * q + 4, :].bitcast(I32)
            )

        def load_atom_scales(q):
            nc.sync.dma_start(
                out=atom_scale[32 * q : 32 * q + 4].bitcast(I32),
                in_=atoms_scales[:, 4 * q : 4 * q + 4, :].rearrange("g r n -> r g n").bitcast(I32),
            )

        def copy_on(on_vector, dst, src):
            if on_vector:
                nc.vector.tensor_copy(out=dst, in_=src)
            else:
                nc.scalar.copy(out=dst, in_=src)

        def level_transpose():
            nc.tensor.transpose(take_bank("level_col")[:].bitcast(BF16)[:, 0:P], level_rows[:], ident16[:])

        def level_columns():
            col_ps = give_bank("level_col")[:].bitcast(BF16)[:, 0:NT]
            nc.scalar.activation(out=level_col[:], in_=col_ps, func=ACT.Identity)

        def load_level_all():
            nc.sync.dma_start(out=level_all[:], in_=level.partition_broadcast(P))

        def enc_interleave(g, u, lo, hi, on_vector):
            src = enc_raw[g][:].rearrange("p j (m u e) -> p u m j e", u=2, e=2)[:, u, lo:hi]
            copy_on(on_vector, enc_b[:, g, u, lo:hi].rearrange("p m e j -> p m j e"), src)

        def quantize(codes, scales, values):
            nc.vector.quantize_mx(out=codes.bitcast(FP8X4), scales=scales, in_=values)

        def enc_quantize(g, u):
            cols = slice(512 * u + 256 * g, 512 * u + 256 * (g + 1))
            values = enc_b[:, g, u].rearrange("p m e j -> p (m e j)")
            quantize(enc_codes[:, cols], enc_scale[:, cols], values)

        def mix_transpose(g, t):
            words = mix_raw[:, g, t, :].bitcast(F32)
            ps = take_bank(("mix", g, t))
            for kg in range(2):
                for u in range(2):
                    n = 2 * kg + u
                    nc.tensor.transpose(ps[:, P * n : P * (n + 1)], words[:, 256 * kg + u : 256 * (kg + 1) : 2], ident32[:])

        def mix_copy(g, t, on_vector=False):
            dst = mix_b[:, g, t].bitcast(F32).rearrange("p (k f u) -> p k f u", k=2, u=2)
            copy_on(on_vector, dst, give_bank(("mix", g, t))[:].rearrange("p (k u f) -> p k f u", k=2, u=2))

        def mix_quantize(g, half):
            slots = slice(2 * half, 2 * half + 2)
            quantize(
                mix_codes[:, g, slots].rearrange("p t n -> p (t n)"),
                mix_scale[:, g, slots].rearrange("p t n -> p (t n)"),
                mix_b[:, g, slots].rearrange("p t n -> p (t n)"),
            )

        def basis_matmul(g, lq):
            ps = take_bank(("basis", g, lq))
            for t in range(4):
                for kg in range(2):
                    nc.tensor.matmul_mx(
                        out=ps[:, P * t : P * (t + 1)],
                        lhsT=mix_codes[:, g, t, P * kg : P * (kg + 1)].bitcast(FP8X4),
                        lhsT_scale=mix_scale[:, g, t, P * kg : P * (kg + 1)],
                        rhs=atom_codes[:, kg, 256 * lq : 256 * (lq + 1)].bitcast(FP4X4),
                        rhs_scale=atom_scale[:, kg, P * lq : P * (lq + 1)],
                        start=(kg == 0),
                        stop=(kg == 1),
                    )

        def basis_copy(g, lq, on_vector=False):
            dst = basis_b[:, g].rearrange("p (s m t) -> p s m t", s=4, t=4)[:, :, 32 * lq : 32 * (lq + 1), :]
            copy_on(on_vector, dst, give_bank(("basis", g, lq))[:].rearrange("p (t m s) -> p s m t", t=4, s=4))

        def basis_quantize(g):
            quantize(basis_codes[:, g], basis_scale[:, g], basis_b[:, g])

        def w_matmul(j, u):
            frames = slice(P * j, P * (j + 1))
            cols = slice(512 * u, 512 * (u + 1))
            nc.tensor.matmul_mx(
                out=take_bank(("w", j, u))[:],
                lhsT=x_codes[:, frames].bitcast(FP8X4),
                lhsT_scale=x_scale[:, frames],
                rhs=enc_codes[:, cols].bitcast(FP8X4),
                rhs_scale=enc_scale[:, cols],
                start=True,
                stop=True,
            )

        def h_tile(j, u):
            if u == 0:
                h_tiles[j] = ring.tile([P, 2, C, 512], BF16, name="h_rows", align_bytes=64)
            return h_tiles[j][:, u].rearrange("p c (m e) -> p c m e", e=2)

        def both_sources(w_half):
            return w_half.rearrange("p (m e) -> p m e", e=2).unsqueeze(1).broadcast_to([P, C, 256, 2])

        def mask_half(j, u):
            return mask_sb[:, j].rearrange("p c (m u e) -> p u c m e", u=2, e=2)[:, u]

        def w_relu(j, u):
            w_tiles[j, u] = ring.tile([P, 512], F32, name="w_sb", bufs=2, align_bytes=64)
            nc.scalar.activation(out=w_tiles[j, u][:], in_=give_bank(("w", j, u))[:], func=ACT.Relu)

        def h_multiply(j, u):
            if (j, u) in ON_GPSIMD:
                nc.gpsimd.tensor_tensor(
                    out=h_tile(j, u), in0=both_sources(w_tiles[j, u][:]), in1=mask_half(j, u), op=ALU.mult
                )
            else:
                nc.vector.scalar_tensor_tensor(
                    out=h_tile(j, u),
                    in0=both_sources(give_bank(("w", j, u))[:]),
                    scalar=0.0,
                    in1=mask_half(j, u),
                    op0=ALU.max,
                    op1=ALU.mult,
                )

        def h_transpose(j, g):
            ps = take_bank(("h", j, g))
            for c in range(C):
                for u in range(2):
                    n = 2 * c + u
                    words = h_tiles[j][:, u, c].bitcast(F32)
                    nc.tensor.transpose(ps[:, P * n : P * (n + 1)], words[:, P * g : P * (g + 1)], ident32[:])

        def h_copy(j, g, on_vector=False):
            pair, half = j // 2, j % 2
            if half == 0:
                ht_tiles[pair, g] = ring.tile([P, 2048], BF16, name="h_cols", bufs=4, align_bytes=64)
            dst = ht_tiles[pair, g][:].bitcast(F32).rearrange("p (c h i u) -> p h c i u", c=C, h=2, u=2)[:, half]
            copy_on(on_vector, dst, give_bank(("h", j, g))[:].rearrange("p (c u i) -> p c i u", c=C, u=2))

        def h_quantize(pair, g):
            quantize(h_codes[:, 2 * pair + g], h_scale[:, 2 * pair + g], ht_tiles[pair, g][:])

        def est_matmul(pair, s):
            ps = take_bank(("est", pair, s))
            for g in range(2):
                nc.tensor.matmul_mx(
                    out=ps[:],
                    lhsT=basis_codes[:, g, P * s : P * (s + 1)].bitcast(FP8X4),
                    lhsT_scale=basis_scale[:, g, P * s : P * (s + 1)],
                    rhs=h_codes[:, 2 * pair + g].bitcast(FP8X4),
                    rhs_scale=h_scale[:, 2 * pair + g],
                    start=(g == 0),
                    stop=(g == 1),
                )

        def z_affine(pair, s, on_vector=False):
            if s == 0:
                z_tiles[pair] = ring.tile([P, 4, C, 256], F32, name="z", bufs=3, align_bytes=64)
            src = give_bank(("est", pair, s))[:]
            dst = z_tiles[pair][:, s].rearrange("p c i -> p (c i)")
            scale, shift = gain32[:, s : s + 1], bias32[:, s : s + 1]
            if on_vector:
                nc.vector.tensor_scalar(out=dst, in0=src, scalar1=scale, scalar2=shift, op0=ALU.mult, op1=ALU.add)
            else:
                nc.scalar.activation(out=dst, in_=src, func=ACT.Identity, scale=scale, bias=shift)

        def y_round(n, lo, hi, on_vector):
            if lo == 0:
                yb_tiles[n] = ring.tile([P, 2, 512], BF16, name="y_b", bufs=4, align_bytes=64)
            first, count = 256 * (n // 2) + P * lo, P * (hi - lo)
            lev = level_all[:, first : first + count]
            dst = yb_tiles[n][:, lo:hi].rearrange("p h k -> p (h k)")
            src = z_tiles[n // 2][:, :, n % 2][:, :, P * lo : P * hi]
            if on_vector:
                nc.vector.tensor_tensor(
                    out=dst.rearrange("p (a i s) -> p a s i", i=2, s=4),
                    in0=src.rearrange("p s (a i) -> p a s i", i=2),
                    in1=lev.rearrange("p (a i) -> p a i", i=2).unsqueeze(2).broadcast_to([P, count // 2, 4, 2]),
                    op=ALU.mult,
                )
            else:
                nc.gpsimd.tensor_tensor(
                    out=dst.rearrange("p (i s) -> p i s", s=4),
                    in0=src.rearrange("p s i -> p i s"),
                    in1=lev.unsqueeze(2).broadcast_to([P, count, 4]),
                    op=ALU.mult,
                )

        def y_quantize(n):
            lo = T * (n % 2) + 256 * (n // 2)
            quantize(y_codes[:, n], y_scale[:, lo : lo + 256], yb_tiles[n][:].rearrange("p h k -> p (h k)"))

        def y_transpose(n, half):
            ps = take_bank(("y", n, half))
            for s in range(4):
                nc.tensor.transpose(ps[:, P * s : P * (s + 1)], z_tiles[n // 2][:, s, n % 2, P * half : P * (half + 1)], ident32[:])

        def y_copy(n, half, on_vector=False):
            if half == 0:
                y_tiles[n] = ring.tile([P, 2, L], F32, name="y_rows", align_bytes=64)
            j = 2 * (n // 2) + half
            dst = y_tiles[n][:, half].rearrange("p (m s) -> p m s", s=4)
            src = give_bank(("y", n, half))[:].rearrange("p (s m) -> p m s", s=4)
            if on_vector:
                nc.vector.tensor_scalar(out=dst, in0=src, scalar1=level_col[:, j : j + 1], scalar2=None, op0=ALU.mult)
            else:
                nc.scalar.activation(out=dst, in_=src, func=ACT.Copy, scale=level_col[:, j : j + 1])

        def store_y(n, lo, hi):
            rows = out_0[n % 2, 256 * (n // 2) : 256 * (n // 2 + 1), :].rearrange("(h i) l -> i h l", h=2)
            nc.sync.dma_start(out=rows[:, lo:hi], in_=y_tiles[n][:, lo:hi])

        def store_codes(pair, lo, hi):
            nc.sync.dma_start(
                out=codes_dram[:, lo:hi, 256 * pair : 256 * (pair + 1)],
                in_=y_codes[:, 2 * pair + lo : 2 * pair + hi].bitcast(I32),
            )

        def ident_cast():
            nc.scalar.activation(out=ident16[:], in_=ident32[:], func=ACT.Identity)

        def warm_up(first):
            ps = take_bank("warm")
            for n in range(first, first + 2):
                nc.tensor.matmul_mx(
                    out=ps[:, 256 * (n % 2) : 256 * (n % 2 + 1)],
                    lhsT=enc_codes[:, 0:P].bitcast(FP8X4),
                    lhsT_scale=enc_scale[:, 0:P],
                    rhs=enc_codes[:, 0:256].bitcast(FP8X4),
                    rhs_scale=enc_scale[:, 0:256],
                    start=True,
                    stop=True,
                )
            give_bank("warm")

        def store_scales(q, eng):
            eng.dma_start(
                out=out_2[0, 4 * q : 4 * q + 4, :].bitcast(I32), in_=y_scale[32 * q : 32 * q + 4, :].bitcast(I32)
            )

        nc.vector.memset(in_scales[:].bitcast(U32), 0)
        nc.vector.memset(level_rows[:], 0.0)
        load_enc(0)
        make_identity(nc, ident32[:])
        load_enc(1)
        nc.gpsimd.dma_start(out=level_rows[0:NT, :], in_=level.rearrange("(j p) -> j p", p=P))
        enc_interleave(0, 0, 0, 128, True)
        nc.gpsimd.dma_start(out=gain_raw[:], in_=gain.rearrange("(p s) -> p s", s=4))
        enc_quantize(0, 0)
        warm_up(0)
        load_x_scales(1)
        enc_interleave(1, 0, 0, 128, True)
        ident_cast()
        enc_interleave(0, 1, 0, 128, False)
        enc_quantize(0, 1)
        enc_quantize(1, 0)
        load_x_scales(0)
        load_x_scales(3)
        warm_up(2)
        load_x_scales(2)
        load_x(0, 256)
        w_matmul(0, 0)
        load_mask(0)
        load_mix(0, 1)
        enc_interleave(1, 1, 0, 128, False)
        enc_quantize(1, 1)
        w_matmul(0, 1)
        w_matmul(1, 0)
        load_mask(1)
        w_matmul(1, 1)
        h_multiply(0, 0)
        load_x(256, 1024)
        load_mix(1, 0)
        mix_transpose(0, 3)
        mix_transpose(0, 2)
        mix_copy(0, 3, False)
        h_multiply(0, 1)
        load_atom_scales(3)
        h_transpose(0, 0)
        h_multiply(1, 0)
        load_atom_scales(1)
        load_atom_scales(0)
        mix_copy(0, 2, False)
        load_mask(2)
        w_matmul(2, 0)
        w_matmul(2, 1)
        level_transpose()
        level_columns()
        load_mix(0, 0)
        h_transpose(0, 1)
        h_multiply(1, 1)
        h_copy(0, 0, False)
        h_copy(0, 1, False)
        mix_transpose(1, 0)
        h_transpose(1, 0)
        mix_transpose(1, 1)
        w_matmul(3, 0)
        w_matmul(3, 1)
        h_transpose(1, 1)
        mix_copy(1, 0, False)
        mix_quantize(0, 1)
        mix_copy(1, 1, False)
        mix_transpose(0, 0)
        h_copy(1, 0, False)
        h_copy(1, 1, False)
        load_atom_scales(2)
        mix_transpose(0, 1)
        h_multiply(2, 0)
        nc.gpsimd.dma_start(out=bias_raw[:], in_=bias.rearrange("(p s) -> p s", s=4))
        load_mask(3)
        h_multiply(2, 1)
        h_transpose(2, 0)
        h_transpose(2, 1)
        load_mix(1, 1)
        mix_copy(0, 0, False)
        mix_copy(0, 1, False)
        load_atoms()
        load_mask(4)
        h_copy(2, 0, False)
        w_matmul(4, 0)
        w_matmul(4, 1)
        mix_transpose(1, 3)
        h_copy(2, 1, False)
        mix_transpose(1, 2)
        mix_copy(1, 3, False)
        h_multiply(3, 0)
        h_multiply(3, 1)
        h_transpose(3, 0)
        load_level_all()
        load_mask(5)
        mix_copy(1, 2, False)
        h_transpose(3, 1)
        h_copy(3, 0, False)
        h_copy(3, 1, False)
        mix_quantize(0, 0)
        basis_matmul(0, 0)
        mix_quantize(1, 0)
        h_quantize(0, 1)
        basis_copy(0, 0, False)
        nc.scalar.activation(out=gain32[:], in_=gain_raw[:], func=ACT.Identity)
        basis_matmul(0, 1)
        mix_quantize(1, 1)
        basis_matmul(1, 0)
        basis_copy(1, 0, False)
        basis_copy(0, 1, False)
        h_multiply(4, 0)
        h_multiply(4, 1)
        load_mask(6)
        basis_matmul(1, 1)
        w_matmul(5, 0)
        basis_matmul(0, 2)
        basis_copy(1, 1, False)
        h_quantize(0, 0)
        basis_copy(0, 2, False)
        w_matmul(5, 1)
        basis_matmul(1, 2)
        basis_matmul(0, 3)
        h_multiply(5, 0)
        basis_copy(1, 2, False)
        basis_matmul(1, 3)
        h_transpose(4, 0)
        h_transpose(4, 1)
        h_multiply(5, 1)
        h_transpose(5, 0)
        h_transpose(5, 1)
        nc.scalar.activation(out=bias32[:], in_=bias_raw[:], func=ACT.Identity)
        basis_copy(0, 3, False)
        basis_quantize(0)
        basis_copy(1, 3, False)
        h_copy(4, 0, False)
        h_copy(4, 1, False)
        load_mask(7)
        h_copy(5, 0, False)
        w_matmul(6, 0)
        basis_quantize(1)
        est_matmul(0, 0)
        h_quantize(1, 0)
        est_matmul(0, 1)
        w_matmul(6, 1)
        est_matmul(0, 2)
        est_matmul(0, 3)
        h_multiply(6, 0)
        h_quantize(1, 1)
        h_copy(5, 1, False)
        h_quantize(2, 1)
        z_affine(0, 0, False)
        z_affine(0, 1, False)
        z_affine(0, 2, False)
        est_matmul(1, 1)
        est_matmul(1, 0)
        h_multiply(6, 1)
        z_affine(0, 3, False)
        y_transpose(0, 0)
        z_affine(1, 0, False)
        z_affine(1, 1, False)
        y_transpose(0, 1)
        y_round(0, 0, 2, True)
        y_transpose(1, 0)
        est_matmul(1, 3)
        est_matmul(1, 2)
        y_transpose(1, 1)
        h_transpose(6, 0)
        y_copy(0, 0, False)
        y_copy(0, 1, False)
        z_affine(1, 2, False)
        h_quantize(2, 0)
        w_matmul(7, 0)
        w_matmul(7, 1)
        z_affine(1, 3, True)
        y_transpose(2, 0)
        y_transpose(3, 0)
        y_copy(1, 0, False)
        y_copy(1, 1, False)
        h_copy(6, 0, False)
        y_round(1, 0, 2, True)
        y_round(2, 0, 2, True)
        h_multiply(7, 0)
        h_multiply(7, 1)
        y_copy(2, 0, False)
        store_y(0, 0, 2)
        y_transpose(2, 1)
        h_transpose(6, 1)
        y_copy(2, 1, False)
        store_y(1, 0, 2)
        h_copy(6, 1, False)
        est_matmul(2, 0)
        est_matmul(2, 1)
        est_matmul(2, 2)
        y_quantize(1)
        z_affine(2, 0, False)
        h_transpose(7, 0)
        z_affine(2, 1, False)
        z_affine(2, 2, False)
        y_round(3, 0, 2, True)
        y_quantize(0)
        y_quantize(3)
        h_transpose(7, 1)
        est_matmul(2, 3)
        h_copy(7, 0, False)
        h_copy(7, 1, True)
        store_y(2, 0, 2)
        store_codes(0, 0, 2)
        h_quantize(3, 0)
        z_affine(2, 3, False)
        y_copy(3, 0, False)
        y_transpose(3, 1)
        y_copy(3, 1, False)
        store_y(3, 0, 2)
        y_transpose(5, 0)
        h_quantize(3, 1)
        y_transpose(4, 0)
        y_quantize(2)
        store_codes(1, 0, 2)
        y_transpose(4, 1)
        y_transpose(5, 1)
        y_copy(4, 0, False)
        y_copy(4, 1, False)
        y_round(4, 0, 2, True)
        est_matmul(3, 1)
        y_copy(5, 0, False)
        est_matmul(3, 0)
        z_affine(3, 0, False)
        z_affine(3, 1, True)
        est_matmul(3, 2)
        store_y(4, 0, 2)
        est_matmul(3, 3)
        z_affine(3, 2, True)
        y_copy(5, 1, False)
        y_round(5, 0, 2, True)
        y_quantize(4)
        z_affine(3, 3, False)
        store_y(5, 0, 2)
        y_quantize(5)
        y_transpose(6, 0)
        y_round(6, 0, 2, True)
        y_round(7, 0, 2, True)
        y_transpose(6, 1)
        y_transpose(7, 0)
        y_copy(6, 0, False)
        y_copy(6, 1, False)
        y_copy(7, 0, False)
        store_codes(2, 0, 2)
        store_y(6, 0, 2)
        y_quantize(6)
        store_y(7, 0, 1)
        y_transpose(7, 1)
        y_quantize(7)
        y_copy(7, 1, False)
        store_y(7, 1, 2)
        store_scales(1, nc.scalar)
        store_scales(2, nc.sync)
        store_codes(3, 0, 2)
        store_scales(3, nc.scalar)
        store_scales(0, nc.sync)
